import numpy as np
import ml_dtypes


def mxq(x, axis, fmt="e4m3"):
    dtype, down = {"e4m3": (ml_dtypes.float8_e4m3fn, 7), "e5m2": (ml_dtypes.float8_e5m2, 14)}[fmt]
    v = np.moveaxis(np.asarray(x, np.float32).astype(ml_dtypes.bfloat16).astype(np.float64), axis, -1)
    blocks = v.reshape(v.shape[:-1] + (-1, 32))
    amax = np.abs(blocks).max(-1, keepdims=True)
    byte = np.maximum(np.where(amax > 0, np.frexp(amax)[1] - 1 + 127, 0) - down, 1)
    scale = np.exp2(byte - 127.0)
    codes = (blocks / scale).astype(np.float32).astype(dtype).astype(np.float64)
    return np.moveaxis((codes * scale).reshape(v.shape), -1, axis)


WIDE = False


def mx_kscale(k):
    if not WIDE:
        return np.ones(k)
    levels = np.array([10, -10, 5, -5, 0])
    if k % 512:
        return np.exp2(np.random.permutation(np.resize(levels, k // 32))).repeat(32)
    a = np.empty((k // 512, 16))
    for p in range(k // 512):
        a[p, :8] = np.random.permutation(np.resize(levels, 8))
        for g in range(8):
            far = levels[np.abs(levels - a[p, g]) >= 10]
            a[p, g + 8] = far[np.random.randint(len(far))]
    return np.exp2(a.ravel()).repeat(32)


BF16 = ml_dtypes.bfloat16


def bf(x):
    return np.asarray(x, np.float32).astype(BF16)


def f64(x):
    return np.asarray(x).astype(np.float64)


B, S, H, C, E = 2, 1024, 512, 256, 512


def logsumexp(v, axis):
    m = v.max(axis=axis, keepdims=True)
    return m + np.log(np.sum(np.exp(v - m), axis=axis, keepdims=True))


def sinkhorn_step(l, lm):
    l = l - logsumexp(l, 2)
    l = l - logsumexp(l, 1) + lm[None, None, :]
    return l


def draw0():
    s, u = mx_kscale(H), mx_kscale(S)
    return {
        "h": bf(np.random.standard_normal((B, S, H)) * s),
        "wp": bf(np.random.standard_normal((H, C)) / np.sqrt(H) / s[:, None]),
        "z": bf(np.log(C) + 1.5 * np.random.standard_normal((B, S))),
        "g": bf(0.03 * np.random.standard_normal((B, S)) * u),
        "f": bf(0.02 * np.random.standard_normal((B, S, E)) / u[:, None]),
    }


def core(h, wp, z, g, f):
    h, wp, z, g, f = f64(h), f64(wp), f64(z), f64(g), f64(f)
    s = h.shape[1]
    c = wp.shape[1]

    t = mxq(h, 2, "e4m3") @ mxq(wp, 0, "e4m3")

    l = np.concatenate([t, z[:, :, None]], axis=-1)

    lm = np.concatenate([np.zeros(c), np.full(1, np.log(s - c))])

    for _ in range(2):
        l = sinkhorn_step(l, lm)

    pg = np.exp(l[:, :, :c]) * g[:, :, None] * np.sqrt(s)

    v = mxq(pg, 1, "e4m3").transpose(0, 2, 1) @ mxq(f, 1, "e4m3")

    y = v / np.sqrt(np.mean(v * v, axis=-1, keepdims=True) + 1e-6)
    return y


def e4m3fn_bytes(y):
    return np.clip(np.asarray(y, np.float64), -448.0, 448.0).astype(np.float32).astype(ml_dtypes.float8_e4m3fn).view(np.uint8)


def e4m3fn_values(b):
    return np.asarray(b, np.uint8).view(ml_dtypes.float8_e4m3fn).astype(np.float64)


def setup_inputs():
    d = draw0()
    x0 = np.asarray(d['h']).astype(np.float64)
    s = (np.max(np.abs(x0), axis=(0, 1), keepdims=True) / 448.0).astype(np.float32)
    out = {}
    for k, v in d.items():
        if k == 'h':
            out['h_bytes'] = e4m3fn_bytes(x0 / s.astype(np.float64))
            out['h_scale'] = s
        else:
            out[k] = v
    return out


def reference(h_bytes, h_scale, wp, z, g, f):
    return core(e4m3fn_values(h_bytes) * h_scale.astype(np.float64), wp, z, g, f)

@@ -1,0 +1,581 @@
+import math
+from contextlib import ExitStack
+
+import concourse.mybir as mybir
+from concourse.masks import make_identity
+
+B, S, H, C, E = 2, 1024, 512, 256, 512
+FLOPS = 2 * B * S * H * C + 2 * B * S * C * E
+
+F32 = mybir.dt.float32
+BF16 = mybir.dt.bfloat16
+U32 = mybir.dt.uint32
+U8 = mybir.dt.uint8
+FP8 = mybir.dt.float8_e4m3fn
+FP8X4 = mybir.dt.float8_e4m3fn_x4
+ALU = mybir.AluOpType
+ACT = mybir.ActivationFunctionType
+AX = mybir.AxisListType
+
+P = 128
+PACK = 4
+PASSES = S // (P * PACK)
+TILES = PASSES * PACK
+PAIRS = TILES // 2
+CHUNKS = C // P
+
+
+def tile_saladsinkhorndustbinaggregation_kernel(tc, h_bytes, h_scale, wp, z, g, f, out):
+    nc = tc.nc
+    with ExitStack() as ctx:
+        sb = ctx.enter_context(tc.tile_pool(name="sb", bufs=1))
+        ps = ctx.enter_context(tc.psum_pool(name="ps", bufs=1))
+
+        def sbt(name, shape, dtype):
+            return sb.tile(shape, dtype, name=name, tag=name, align_bytes=64)
+
+        def bank(tag, name, shape):
+            return ps.tile(shape, F32, name=name, tag=tag)
+
+        def spread(col):
+            return col.to_broadcast([P, P])
+
+        hs = sbt("hs", [P, PACK], F32)
+        nc.sync.dma_start(out=hs[:], in_=h_scale.rearrange("a o (p t) -> p (a o t)", t=PACK))
+        hbytes = {}
+
+        def load_h(b, q):
+            hbytes[b, q] = sbt("hbytes%d%d" % (b, q), [P, PACK * H], U8)
+            nc.sync.dma_start(
+                out=hbytes[b, q][:],
+                in_=h_bytes[b, q * P * PACK : (q + 1) * P * PACK, :].rearrange("(p j) k -> p (j k)", j=PACK),
+            )
+
+        fraw = {}
+
+        def load_f(b, q):
+            fraw[b, q] = sbt("fraw%d%d" % (b, q), [P, PACK, E], BF16)
+            nc.sync.dma_start(
+                out=fraw[b, q][:],
+                in_=f[b, q * P * PACK : (q + 1) * P * PACK, :].rearrange("(p j) e -> p j e", j=PACK),
+            )
+
+        load_h(0, 0)
+        wraw = sbt("wraw", [P, PACK, C], BF16)
+        nc.sync.dma_start(out=wraw[:], in_=wp.rearrange("(p j) c -> p j c", j=PACK))
+        load_h(0, 1)
+        zraw = sbt("zraw", [P, B * PASSES, PACK], BF16)
+        nc.sync.dma_start(out=zraw[:], in_=z.rearrange("b (q p j) -> p (b q) j", p=P, j=PACK))
+        load_f(0, 0)
+        load_h(1, 0)
+        load_h(1, 1)
+        load_f(0, 1)
+        graw = sbt("graw", [P, B * PASSES, PACK], BF16)
+        nc.sync.dma_start(out=graw[:], in_=g.rearrange("b (q p j) -> p (b q) j", p=P, j=PACK))
+        load_f(1, 0)
+        load_f(1, 1)
+
+        ident = sbt("ident", [P, P], F32)
+        make_identity(nc, ident[:])
+
+        sc_ps = bank("S1", "sc_ps", [P, PACK, P])
+        for t in range(PACK):
+            nc.tensor.transpose(sc_ps[:, t, :], spread(hs[:, t : t + 1]), ident[:])
+        scale_rows = sbt("scale_rows", [P, H], F32)
+        nc.scalar.activation(
+            out=scale_rows[:].rearrange("m (p t) -> m p t", t=PACK),
+            in_=sc_ps[:].rearrange("m t p -> m p t"),
+            func=ACT.Copy,
+        )
+
+        negz = sbt("negz", [P, B * TILES], F32)
+        nc.gpsimd.tensor_scalar(
+            out=negz[:], in0=zraw[:].rearrange("p a j -> p (a j)"), scalar1=-1.0, scalar2=0.0, op0=ALU.mult, op1=ALU.add
+        )
+        gate = sbt("gate", [P, B * TILES], F32)
+        nc.gpsimd.tensor_scalar(
+            out=gate[:], in0=graw[:].rearrange("p a j -> p (a j)"), scalar1=math.sqrt(S), scalar2=0.0, op0=ALU.mult, op1=ALU.add
+        )
+
+        w_codes = sbt("w_codes", [P, C], U32)
+        w_scales = sbt("w_scales", [P, C], U8)
+        wgrp = sbt("wgrp", [P, C, PACK], BF16)
+
+        def w_group():
+            nc.scalar.copy(out=wgrp[:], in_=wraw[:].rearrange("p j c -> p c j"))
+
+        def w_quant():
+            nc.vector.quantize_mx(out=w_codes[:].bitcast(FP8X4), scales=w_scales[:], in_=wgrp[:].rearrange("p c j -> p (c j)"))
+
+        hwide, hgrp, h_codes, h_scales, scores = {}, {}, {}, {}, {}
+
+        def h_widen(b, i):
+            q, j = divmod(i, PACK)
+            hwide[b, i] = sbt("hwide%d%d" % (b, i), [P, H], BF16)
+            nc.vector.tensor_tensor(
+                out=hwide[b, i][:], in0=hbytes[b, q][:, j * H : (j + 1) * H].bitcast(FP8), in1=scale_rows[:], op=ALU.mult
+            )
+
+        def h_turn(b, k):
+            turned = bank("H%d" % (k % 2), "turned%d%d" % (b, k), [P, 2, 2, P])
+            for jj in range(2):
+                words = hwide[b, 2 * k + jj][:].bitcast(F32)
+                for u in range(2):
+                    nc.tensor.transpose(turned[:, jj, u, :], words[:, u : H // 2 : 2], ident[:])
+            hgrp[b, k] = sbt("hgrp%d%d" % (b, k), [P, 2 * P * PACK], BF16)
+            nc.scalar.copy(
+                out=hgrp[b, k][:].bitcast(F32).rearrange("p (a r u) -> p a r u", a=2, u=2),
+                in_=turned[:].rearrange("p a u r -> p a r u"),
+            )
+
+        def h_quant(b, k):
+            h_codes[b, k] = sbt("h_codes%d%d" % (b, k), [P, 2 * P], U32)
+            h_scales[b, k] = sbt("h_scales%d%d" % (b, k), [P, 2 * P], U8)
+            nc.vector.quantize_mx(out=h_codes[b, k][:].bitcast(FP8X4), scales=h_scales[b, k][:], in_=hgrp[b, k][:])
+
+        def score_matmul(b, k):
+            scores[b, k] = bank("T%d" % k, "scores%d%d" % (b, k), [P, 2, C])
+            for jj in range(2):
+                cols = slice(jj * P, (jj + 1) * P)
+                nc.tensor.matmul_mx(
+                    out=scores[b, k][:, jj, :],
+                    lhsT=h_codes[b, k][:, cols].bitcast(FP8X4),
+                    lhsT_scale=h_scales[b, k][:, cols],
+                    rhs=w_codes[:].bitcast(FP8X4),
+                    rhs_scale=w_scales[:],
+                    start=True,
+                    stop=True,
+                )
+
+        fgrp, f_codes, f_scales = {}, {}, {}
+
+        def f_group(b, q, half):
+            if half == 0:
+                fgrp[b, q] = sbt("fgrp%d%d" % (b, q), [P, E, PACK], BF16)
+            cols = slice(half * E // 2, (half + 1) * E // 2)
+            nc.scalar.copy(out=fgrp[b, q][:, cols, :], in_=fraw[b, q][:, :, cols].rearrange("p j e -> p e j"))
+
+        def f_quant(b, q):
+            f_codes[b, q] = sbt("f_codes%d%d" % (b, q), [P, E], U32)
+            f_scales[b, q] = sbt("f_scales%d%d" % (b, q), [P, E], U8)
+            nc.vector.quantize_mx(
+                out=f_codes[b, q][:].bitcast(FP8X4), scales=f_scales[b, q][:], in_=fgrp[b, q][:].rearrange("p e j -> p (e j)")
+            )
+
+        def per_batch(name, shape, dtype=F32):
+            return [sbt("%s%d" % (name, b), shape, dtype) for b in range(B)]
+
+        rowmax = per_batch("rowmax", [P, TILES])
+        negm = per_batch("negm", [P, TILES])
+        rowsum1 = per_batch("rowsum1", [P, TILES])
+        zgap = per_batch("zgap", [P, TILES])
+        zgap_min = per_batch("zgap_min", [P, 1])
+        zgap_least = per_batch("zgap_least", [P, 1])
+        ez_row = per_batch("ez_row", [P, TILES])
+        ez_col = per_batch("ez_col", [P, TILES])
+        total1 = per_batch("total1", [P, TILES])
+        u1 = per_batch("u1", [P, TILES])
+        zprod = per_batch("zprod", [P, TILES])
+        zpart = per_batch("zpart", [P, 1])
+        acc = [per_batch("acc_even", [P, C]), per_batch("acc_odd", [P, C])]
+        colmax = per_batch("colmax", [P, CHUNKS])
+        colmax_rows = per_batch("colmax_rows", [P, C])
+        kern = per_batch("kern", [P, TILES, C + PACK])
+        rowsum2 = per_batch("rowsum2", [P, TILES])
+        u2 = per_batch("u2", [P, TILES])
+        junk_s = per_batch("junk_s", [P, TILES, C], BF16)
+        junk_v = per_batch("junk_v", [P, TILES, C + PACK], BF16)
+        junk_q = per_batch("junk_q", [P, CHUNKS, E], BF16)
+        shifted = {}
+
+        def row_max(b, k):
+            nc.vector.tensor_reduce(out=rowmax[b][:, 2 * k : 2 * k + 2], in_=scores[b, k][:], axis=AX.X, op=ALU.max)
+
+        def row_shift(b, q):
+            cols = slice(q * PACK, (q + 1) * PACK)
+            nc.vector.scalar_tensor_tensor(
+                out=negm[b][:, cols],
+                in0=rowmax[b][:, cols],
+                scalar=-1.0,
+                in1=negz[:, b * TILES + q * PACK : b * TILES + (q + 1) * PACK],
+                op0=ALU.mult,
+                op1=ALU.min,
+            )
+
+        def row_sum1(b, i):
+            nc.scalar.activation(
+                out=junk_s[b][:, i, :],
+                in_=scores[b, i // 2][:, i % 2, :],
+                func=ACT.Exp,
+                bias=negm[b][:, i : i + 1],
+                accum_out=rowsum1[b][:, i : i + 1],
+            )
+
+        def dust_gap(b):
+            nc.gpsimd.tensor_tensor(out=zgap[b][:], in0=negz[:, b * TILES : (b + 1) * TILES], in1=negm[b][:], op=ALU.subtract)
+
+        zturned = {}
+
+        def dust_min(b):
+            nc.vector.tensor_reduce(out=zgap_min[b][:], in_=zgap[b][:], axis=AX.X, op=ALU.min)
+            zturned[b] = bank("S%d" % b, "zt%d" % b, [P, P])
+            nc.tensor.transpose(zturned[b][:], spread(zgap_min[b][:]), ident[:])
+
+        def dust_shift(b):
+            nc.vector.tensor_reduce(out=zgap_least[b][:], in_=zturned[b][:], axis=AX.X, op=ALU.min)
+
+        def dust_exp(b):
+            nc.scalar.activation(out=ez_row[b][:], in_=zgap[b][:], func=ACT.Exp, scale=-1.0)
+            nc.scalar.activation(out=ez_col[b][:], in_=zgap[b][:], func=ACT.Exp, scale=-1.0, bias=zgap_least[b][:])
+
+        def row_total1(b):
+            nc.gpsimd.tensor_tensor(out=total1[b][:], in0=rowsum1[b][:], in1=ez_row[b][:], op=ALU.add)
+
+        def col_max_step(b, i):
+            src = scores[b, i // 2][:, i % 2, :]
+            dst = acc[i % 2][b]
+            if i < 2:
+                nc.vector.tensor_scalar(out=dst[:], in0=src, scalar1=negm[b][:, i : i + 1], scalar2=None, op0=ALU.add)
+            else:
+                nc.vector.scalar_tensor_tensor(
+                    out=dst[:], in0=src, scalar=negm[b][:, i : i + 1], in1=dst[:], op0=ALU.add, op1=ALU.max
+                )
+
+        acc_turned = {}
+
+        def col_max_turn(b, par):
+            if par == 0:
+                acc_turned[b] = bank("S%d" % b, "acc_turned%d" % b, [P, CHUNKS, 2, P])
+            for ch in range(CHUNKS):
+                nc.tensor.transpose(acc_turned[b][:, ch, par, :], acc[par][b][:, ch * P : (ch + 1) * P], ident[:])
+
+        def col_max_finish(b):
+            nc.vector.tensor_reduce(
+                out=colmax[b][:], in_=acc_turned[b][:].rearrange("p c a r -> p c (a r)"), axis=AX.X, op=ALU.max
+            )
+            rows = spread_columns(b, "colmax_ps%d" % b, [colmax[b][:, ch : ch + 1] for ch in range(CHUNKS)])
+            nc.scalar.copy(out=colmax_rows[b][:], in_=rows[:])
+
+        def spread_columns(b, name, cols):
+            rows = bank("S%d" % b, name, [P, len(cols) * P])
+            for ch in range(len(cols)):
+                nc.tensor.transpose(rows[:, ch * P : (ch + 1) * P], spread(cols[ch]), ident[:])
+            return rows
+
+        def row_weights1(b):
+            nc.vector.reciprocal(out=u1[b][:], in_=total1[b][:])
+
+        def dust_partial(b):
+            nc.vector.scalar_tensor_tensor(
+                out=zprod[b][:], in0=ez_col[b][:], scalar=1.0, in1=u1[b][:], op0=ALU.mult, op1=ALU.mult, accum_out=zpart[b][:]
+            )
+            nc.scalar.activation(out=kern[b][:, :, C], in_=zprod[b][:], func=ACT.Copy, scale=float(S - C))
+
+        def col_shift(b, k):
+            shifted[b, k] = sbt("shifted%d%d" % (b, k), [P, 2, C], F32)
+            nc.vector.tensor_tensor(
+                out=shifted[b, k][:],
+                in0=scores[b, k][:],
+                in1=colmax_rows[b][:].unsqueeze(1).to_broadcast([P, 2, C]),
+                op=ALU.subtract,
+            )
+
+        def kernel_exp(b, i):
+            nc.scalar.activation(
+                out=kern[b][:, i, 0:C], in_=shifted[b, i // 2][:, i % 2, :], func=ACT.Exp, bias=negm[b][:, i : i + 1]
+            )
+
+        sums = {}
+
+        def scale_rows_by(b, r, i, on_scalar):
+            weights = u1[b] if r == 1 else u2[b]
+            tile = kern[b][:, i, 0:C]
+            if on_scalar:
+                nc.scalar.activation(out=tile, in_=tile, func=ACT.Copy, scale=weights[:, i : i + 1])
+            else:
+                nc.vector.tensor_scalar(out=tile, in0=tile, scalar1=weights[:, i : i + 1], scalar2=None, op0=ALU.mult)
+
+        def col_sum_open(b, r):
+            sums[b, r] = [bank("H%d" % ch, "colsum%d%d%d" % (b, r, ch), [P, 2, P]) for ch in range(CHUNKS)]
+            if r == 1:
+                nc.tensor.transpose(sums[b, r][0][:, 0, :], spread(zpart[b][:]), ident[:])
+
+        def col_sum_step(b, r, i):
+            for ch in range(CHUNKS):
+                nc.tensor.matmul(
+                    sums[b, r][ch][:, 1, :],
+                    lhsT=kern[b][:, i, ch * P : (ch + 1) * P],
+                    rhs=ident[:],
+                    start=(i == 0),
+                    stop=(i == TILES - 1),
+                    is_transpose=True,
+                )
+
+        vrows, csum, vcol = {}, {}, {}
+
+        def col_total(b, r):
+            first = 0 if r == 1 else 1
+            csum[b, r] = sbt("csum%d%d" % (b, r), [P, 3], F32)
+            nc.vector.tensor_reduce(out=csum[b, r][:, first:2], in_=sums[b, r][0][:, first:2, :], axis=AX.X, op=ALU.add)
+            nc.vector.tensor_reduce(out=csum[b, r][:, 2:3], in_=sums[b, r][1][:, 1:2, :], axis=AX.X, op=ALU.add)
+
+        def col_weights(b, r):
+            first = 0 if r == 1 else 1
+            vcol = sbt("vcol%d%d" % (b, r), [P, 3], F32)
+            nc.vector.reciprocal(out=vcol[:, first:3], in_=csum[b, r][:, first:3])
+            cols = [vcol[:, 1:2], vcol[:, 2:3]] + ([vcol[:, 0:1]] if r == 1 else [])
+            vrows[b, r] = spread_columns(b, "vrows%d%d" % (b, r), cols)
+
+        def row_sum2(b, i):
+            nc.vector.scalar_tensor_tensor(
+                out=junk_v[b][:, i, 0 : C + 1],
+                in0=kern[b][:, i, 0 : C + 1],
+                scalar=1.0,
+                in1=vrows[b, 1][:, 0 : C + 1],
+                op0=ALU.mult,
+                op1=ALU.mult,
+                accum_out=rowsum2[b][:, i : i + 1],
+            )
+
+        def row_weights2(b, lo, hi):
+            nc.vector.reciprocal(out=u2[b][:, lo:hi], in_=rowsum2[b][:, lo:hi])
+
+        pg, pgrp, p_codes, p_scales = {}, {}, {}, {}
+
+        def assign(b, i):
+            q, j = divmod(i, PACK)
+            if j == 0:
+                pg[b, q] = sbt("pg%d%d" % (b, q), [P, PACK, C], BF16)
+            nc.vector.scalar_tensor_tensor(
+                out=pg[b, q][:, j, :],
+                in0=kern[b][:, i, 0:C],
+                scalar=gate[:, b * TILES + i : b * TILES + i + 1],
+                in1=vrows[b, 2][:],
+                op0=ALU.mult,
+                op1=ALU.mult,
+            )
+
+        def p_group(b, q, on_scalar):
+            pgrp[b, q] = sbt("pgrp%d%d" % (b, q), [P, C, PACK], BF16)
+            if on_scalar:
+                nc.scalar.copy(out=pgrp[b, q][:], in_=pg[b, q][:].rearrange("p j c -> p c j"))
+            else:
+                nc.vector.tensor_copy(out=pgrp[b, q][:], in_=pg[b, q][:].rearrange("p j c -> p c j"))
+
+        def p_quant(b, q):
+            p_codes[b, q] = sbt("p_codes%d%d" % (b, q), [P, C], U32)
+            p_scales[b, q] = sbt("p_scales%d%d" % (b, q), [P, C], U8)
+            nc.vector.quantize_mx(
+                out=p_codes[b, q][:].bitcast(FP8X4), scales=p_scales[b, q][:], in_=pgrp[b, q][:].rearrange("p c j -> p (c j)")
+            )
+
+        agg = {}
+
+        def aggregate(b, q):
+            for ch in range(CHUNKS):
+                if q == 0:
+                    agg[b, ch] = bank("T%d" % (CHUNKS * b + ch), "agg%d%d" % (b, ch), [P, E])
+                cols = slice(ch * P, (ch + 1) * P)
+                nc.tensor.matmul_mx(
+                    out=agg[b, ch][:],
+                    lhsT=p_codes[b, q][:, cols].bitcast(FP8X4),
+                    lhsT_scale=p_scales[b, q][:, cols],
+                    rhs=f_codes[b, q][:].bitcast(FP8X4),
+                    rhs_scale=f_scales[b, q][:],
+                    start=(q == 0),
+                    stop=(q == PASSES - 1),
+                )
+
+        root, inv = {}, {}
+
+        def norm_root(b, ch):
+            sq = sbt("sq%d%d" % (b, ch), [P, 1], F32)
+            root[b, ch] = sbt("root%d%d" % (b, ch), [P, 1], F32)
+            nc.scalar.activation(out=junk_q[b][:, ch, :], in_=agg[b, ch][:], func=ACT.Square, accum_out=sq[:])
+            nc.scalar.activation(out=root[b, ch][:], in_=sq[:], func=ACT.Sqrt, scale=1.0 / E, bias=1e-6)
+
+        def norm_inverse(b, ch):
+            inv[b, ch] = sbt("inv%d%d" % (b, ch), [P, 1], F32)
+            nc.vector.reciprocal(out=inv[b, ch][:], in_=root[b, ch][:])
+
+        def store(b, ch, on_scalar):
+            y = sbt("y%d%d" % (b, ch), [P, E], F32)
+            if on_scalar:
+                nc.scalar.activation(out=y[:], in_=agg[b, ch][:], func=ACT.Copy, scale=inv[b, ch][:])
+            else:
+                nc.vector.tensor_scalar(out=y[:], in0=agg[b, ch][:], scalar1=inv[b, ch][:], scalar2=None, op0=ALU.mult)
+            nc.sync.dma_start(out=out[b, ch * P : (ch + 1) * P, :], in_=y[:])
+
+        ctx.enter_context(tc.manual_schedule())
+
+        w_group()
+        for k in range(PAIRS):
+            h_widen(0, 2 * k)
+            if k == 1:
+                w_quant()
+            if k > 1:
+                h_quant(0, k - 2)
+                score_matmul(0, k - 2)
+            h_widen(0, 2 * k + 1)
+            h_turn(0, k)
+            if k > 1:
+                f_group(0, 0, k - 2)
+        h_widen(1, 0)
+        h_quant(0, 2)
+        score_matmul(0, 2)
+        row_max(0, 0)
+        h_quant(0, 3)
+        score_matmul(0, 3)
+        row_max(0, 1)
+        h_widen(1, 1)
+        h_turn(1, 0)
+        f_group(0, 1, 0)
+        row_shift(0, 0)
+        row_max(0, 2)
+        row_max(0, 3)
+        h_widen(1, 2)
+        row_shift(0, 1)
+        dust_gap(0)
+        for i in range(TILES):
+            col_max_step(0, i)
+            row_sum1(0, (i + 2) % TILES)
+            if i == 2:
+                dust_min(0)
+            if i == 5:
+                dust_shift(0)
+            if i >= TILES - 2:
+                col_max_turn(0, i % 2)
+        dust_exp(0)
+        row_total1(0)
+        h_widen(1, 3)
+        h_turn(1, 1)
+        h_widen(1, 4)
+        col_max_finish(0)
+        h_widen(1, 5)
+        h_turn(1, 2)
+        row_weights1(0)
+        h_widen(1, 6)
+        dust_partial(0)
+        h_widen(1, 7)
+        h_turn(1, 3)
+        f_group(0, 1, 1)
+        h_quant(1, 0)
+        col_sum_open(0, 1)
+        for k in range(PAIRS):
+            col_shift(0, k)
+            if k < PAIRS - 1:
+                h_quant(1, k + 1)
+            score_matmul(1, k)
+            kernel_exp(0, 2 * k)
+            kernel_exp(0, 2 * k + 1)
+            if True:
+                for i in (2 * k, 2 * k + 1):
+                    scale_rows_by(0, 1, i, True)
+                    col_sum_step(0, 1, i)
+        for k in range(PAIRS):
+            row_max(1, k)
+            if k == 2:
+                row_shift(1, 0)
+            if not True:
+                for i in (2 * k, 2 * k + 1):
+                    scale_rows_by(0, 1, i, False)
+                    col_sum_step(0, 1, i)
+        f_quant(0, 0)
+        row_shift(1, 1)
+        dust_gap(1)
+        for i in range(TILES):
+            col_max_step(1, i)
+            row_sum1(1, (i + 2) % TILES)
+            if i == 1:
+                col_total(0, 1)
+            if i == 2:
+                dust_min(1)
+            if i == 3:
+                col_weights(0, 1)
+            if i == 5:
+                dust_shift(1)
+            if i >= TILES - 2:
+                col_max_turn(1, i % 2)
+        dust_exp(1)
+        row_total1(1)
+        f_group(1, 0, 0)
+        col_sum_open(0, 2)
+        for i in range(TILES):
+            row_sum2(0, i)
+            if i == 2:
+                col_max_finish(1)
+            if i == PACK:
+                row_weights2(0, 0, PACK)
+                for ii in range(PACK):
+                    scale_rows_by(0, 2, ii, True)
+                    col_sum_step(0, 2, ii)
+            if i == 5:
+                row_weights1(1)
+        dust_partial(1)
+        row_weights2(0, PACK, TILES)
+        for ii in range(PACK, TILES):
+            scale_rows_by(0, 2, ii, True)
+            col_sum_step(0, 2, ii)
+        for k in range(PAIRS):
+            col_shift(1, k)
+            kernel_exp(1, 2 * k)
+            kernel_exp(1, 2 * k + 1)
+            if k == 2:
+                col_total(0, 2)
+        col_weights(0, 2)
+        f_quant(0, 1)
+        col_sum_open(1, 1)
+        for i in range(TILES):
+            scale_rows_by(1, 1, i, True)
+            col_sum_step(1, 1, i)
+        for i in range(TILES):
+            assign(0, i)
+            if i == PACK - 1:
+                p_group(0, 0, True)
+            if i == 5:
+                col_total(1, 1)
+        col_weights(1, 1)
+        p_group(0, 1, True)
+        f_group(1, 0, 1)
+        p_quant(0, 0)
+        aggregate(0, 0)
+        col_sum_open(1, 2)
+        for i in range(TILES):
+            row_sum2(1, i)
+            if i == 2:
+                p_quant(0, 1)
+                aggregate(0, 1)
+            if i == PACK:
+                row_weights2(1, 0, PACK)
+                for ii in range(PACK):
+                    scale_rows_by(1, 2, ii, True)
+                    col_sum_step(1, 2, ii)
+        row_weights2(1, PACK, TILES)
+        for ii in range(PACK, TILES):
+            scale_rows_by(1, 2, ii, True)
+            col_sum_step(1, 2, ii)
+        f_quant(1, 0)
+        f_group(1, 1, 0)
+        f_group(1, 1, 1)
+        col_total(1, 2)
+        col_weights(1, 2)
+        norm_root(0, 0)
+        norm_root(0, 1)
+        f_quant(1, 1)
+        for i in range(TILES):
+            assign(1, i)
+            if i == PACK - 1:
+                p_group(1, 0, True)
+        p_group(1, 1, False)
+        p_quant(1, 0)
+        aggregate(1, 0)
+        p_quant(1, 1)
+        aggregate(1, 1)
+        for ch in range(CHUNKS):
+            norm_inverse(0, ch)
+            store(0, ch, False)
+        for ch in range(CHUNKS):
+            norm_root(1, ch)
+        for ch in range(CHUNKS):
+            norm_inverse(1, ch)
+            store(1, ch, ch == 0)

@@ -9,6 +9,7 @@ FLOPS = 2 * B * S * H * C + 2 * B * S * C * E
 
 F32 = mybir.dt.float32
 BF16 = mybir.dt.bfloat16
+I32 = mybir.dt.int32
 U32 = mybir.dt.uint32
 U8 = mybir.dt.uint8
 FP8 = mybir.dt.float8_e4m3fn
@@ -19,10 +20,12 @@ AX = mybir.AxisListType
 
 P = 128
 PACK = 4
-PASSES = S // (P * PACK)
+SPAN = P * PACK
+PASSES = S // SPAN
 TILES = PASSES * PACK
 PAIRS = TILES // 2
 CHUNKS = C // P
+LN2 = math.log(2.0)
 
 
 def tile_saladsinkhorndustbinaggregation_kernel(tc, h_bytes, h_scale, wp, z, g, f, out):
@@ -30,55 +33,56 @@ def tile_saladsinkhorndustbinaggregation_kernel(tc, h_bytes, h_scale, wp, z, g, 
     with ExitStack() as ctx:
         sb = ctx.enter_context(tc.tile_pool(name="sb", bufs=1))
         ps = ctx.enter_context(tc.psum_pool(name="ps", bufs=1))
+        ctx.enter_context(tc.manual_schedule())
 
         def sbt(name, shape, dtype):
             return sb.tile(shape, dtype, name=name, tag=name, align_bytes=64)
 
-        def bank(tag, name, shape):
-            return ps.tile(shape, F32, name=name, tag=tag)
+        def bank(n, name, shape):
+            return ps.tile(shape, F32, name=name, tag="bank%d" % n)
 
         def spread(col):
             return col.to_broadcast([P, P])
 
+        def per_batch(name, shape, dtype=F32):
+            return [sbt("%s%d" % (name, b), shape, dtype) for b in range(B)]
+
         hs = sbt("hs", [P, PACK], F32)
         nc.sync.dma_start(out=hs[:], in_=h_scale.rearrange("a o (p t) -> p (a o t)", t=PACK))
-        hbytes = {}
+        hbytes, fraw = {}, {}
 
         def load_h(b, q):
-            hbytes[b, q] = sbt("hbytes%d%d" % (b, q), [P, PACK * H], U8)
+            hbytes[b, q] = sbt("hbytes%d%d" % (b, q), [P, 2, 2 * H], U8)
             nc.sync.dma_start(
                 out=hbytes[b, q][:],
-                in_=h_bytes[b, q * P * PACK : (q + 1) * P * PACK, :].rearrange("(p j) k -> p (j k)", j=PACK),
+                in_=h_bytes[b, q * SPAN : (q + 1) * SPAN, :].rearrange("(a p j) k -> p a (j k)", a=2, j=2),
             )
-
-        fraw = {}
 
         def load_f(b, q):
             fraw[b, q] = sbt("fraw%d%d" % (b, q), [P, PACK, E], BF16)
             nc.sync.dma_start(
-                out=fraw[b, q][:],
-                in_=f[b, q * P * PACK : (q + 1) * P * PACK, :].rearrange("(p j) e -> p j e", j=PACK),
+                out=fraw[b, q][:], in_=f[b, q * SPAN : (q + 1) * SPAN, :].rearrange("(p j) e -> p j e", j=PACK)
             )
 
-        load_h(0, 0)
         wraw = sbt("wraw", [P, PACK, C], BF16)
         nc.sync.dma_start(out=wraw[:], in_=wp.rearrange("(p j) c -> p j c", j=PACK))
+        load_h(0, 0)
         load_h(0, 1)
-        zraw = sbt("zraw", [P, B * PASSES, PACK], BF16)
-        nc.sync.dma_start(out=zraw[:], in_=z.rearrange("b (q p j) -> p (b q) j", p=P, j=PACK))
+        zraw = sbt("zraw", [P, B * PASSES * 2, 2], BF16)
+        nc.sync.dma_start(out=zraw[:], in_=z.rearrange("b (a p j) -> p (b a) j", p=P, j=2))
         load_f(0, 0)
+        load_f(0, 1)
         load_h(1, 0)
         load_h(1, 1)
-        load_f(0, 1)
-        graw = sbt("graw", [P, B * PASSES, PACK], BF16)
-        nc.sync.dma_start(out=graw[:], in_=g.rearrange("b (q p j) -> p (b q) j", p=P, j=PACK))
         load_f(1, 0)
         load_f(1, 1)
+        graw = sbt("graw", [P, B * PASSES * 2, 2], BF16)
+        nc.sync.dma_start(out=graw[:], in_=g.rearrange("b (a p j) -> p (b a) j", p=P, j=2))
 
         ident = sbt("ident", [P, P], F32)
         make_identity(nc, ident[:])
 
-        sc_ps = bank("S1", "sc_ps", [P, PACK, P])
+        sc_ps = bank(7, "sc_ps", [P, PACK, P])
         for t in range(PACK):
             nc.tensor.transpose(sc_ps[:, t, :], spread(hs[:, t : t + 1]), ident[:])
         scale_rows = sbt("scale_rows", [P, H], F32)
@@ -88,44 +92,51 @@ def tile_saladsinkhorndustbinaggregation_kernel(tc, h_bytes, h_scale, wp, z, g, 
             func=ACT.Copy,
         )
 
-        negz = sbt("negz", [P, B * TILES], F32)
-        nc.gpsimd.tensor_scalar(
-            out=negz[:], in0=zraw[:].rearrange("p a j -> p (a j)"), scalar1=-1.0, scalar2=0.0, op0=ALU.mult, op1=ALU.add
-        )
-        gate = sbt("gate", [P, B * TILES], F32)
-        nc.gpsimd.tensor_scalar(
-            out=gate[:], in0=graw[:].rearrange("p a j -> p (a j)"), scalar1=math.sqrt(S), scalar2=0.0, op0=ALU.mult, op1=ALU.add
-        )
+        def by_tile(name, raw, factor):
+            dst = sbt(name, [P, B * TILES], F32)
+            nc.gpsimd.tensor_scalar(
+                out=dst[:].rearrange("p (q j a) -> p q j a", j=2, a=2),
+                in0=raw[:].rearrange("p (q a) j -> p q j a", a=2),
+                scalar1=factor,
+                scalar2=0.0,
+                op0=ALU.mult,
+                op1=ALU.add,
+            )
+            return dst
+
+        negz = by_tile("negz", zraw, -1.0)
 
         w_codes = sbt("w_codes", [P, C], U32)
         w_scales = sbt("w_scales", [P, C], U8)
         wgrp = sbt("wgrp", [P, C, PACK], BF16)
 
         def w_group():
-            nc.scalar.copy(out=wgrp[:], in_=wraw[:].rearrange("p j c -> p c j"))
+            nc.vector.tensor_copy(out=wgrp[:], in_=wraw[:].rearrange("p j c -> p c j"))
 
         def w_quant():
             nc.vector.quantize_mx(out=w_codes[:].bitcast(FP8X4), scales=w_scales[:], in_=wgrp[:].rearrange("p c j -> p (c j)"))
 
-        hwide, hgrp, h_codes, h_scales, scores = {}, {}, {}, {}, {}
+        hwide, hturn, hgrp, h_codes, h_scales, scores = {}, {}, {}, {}, {}, {}
 
         def h_widen(b, i):
-            q, j = divmod(i, PACK)
+            q, j, a = i // PACK, (i // 2) % 2, i % 2
             hwide[b, i] = sbt("hwide%d%d" % (b, i), [P, H], BF16)
             nc.vector.tensor_tensor(
-                out=hwide[b, i][:], in0=hbytes[b, q][:, j * H : (j + 1) * H].bitcast(FP8), in1=scale_rows[:], op=ALU.mult
+                out=hwide[b, i][:], in0=hbytes[b, q][:, a, j * H : (j + 1) * H].bitcast(FP8), in1=scale_rows[:], op=ALU.mult
             )
 
         def h_turn(b, k):
-            turned = bank("H%d" % (k % 2), "turned%d%d" % (b, k), [P, 2, 2, P])
+            hturn[b, k] = bank(4 + k % 2, "turned%d%d" % (b, k), [P, 2, 2, P])
             for jj in range(2):
                 words = hwide[b, 2 * k + jj][:].bitcast(F32)
                 for u in range(2):
-                    nc.tensor.transpose(turned[:, jj, u, :], words[:, u : H // 2 : 2], ident[:])
-            hgrp[b, k] = sbt("hgrp%d%d" % (b, k), [P, 2 * P * PACK], BF16)
+                    nc.tensor.transpose(hturn[b, k][:, jj, u, :], words[:, u : H // 2 : 2], ident[:])
+
+        def h_group(b, k):
+            hgrp[b, k] = sbt("hgrp%d%d" % (b, k), [P, 2 * SPAN], BF16)
             nc.scalar.copy(
                 out=hgrp[b, k][:].bitcast(F32).rearrange("p (a r u) -> p a r u", a=2, u=2),
-                in_=turned[:].rearrange("p a u r -> p a r u"),
+                in_=hturn[b, k][:].rearrange("p a u r -> p a r u"),
             )
 
         def h_quant(b, k):
@@ -134,7 +145,7 @@ def tile_saladsinkhorndustbinaggregation_kernel(tc, h_bytes, h_scale, wp, z, g, 
             nc.vector.quantize_mx(out=h_codes[b, k][:].bitcast(FP8X4), scales=h_scales[b, k][:], in_=hgrp[b, k][:])
 
         def score_matmul(b, k):
-            scores[b, k] = bank("T%d" % k, "scores%d%d" % (b, k), [P, 2, C])
+            scores[b, k] = bank(6 + k % 2, "scores%d%d" % (b, k), [P, 2, C])
             for jj in range(2):
                 cols = slice(jj * P, (jj + 1) * P)
                 nc.tensor.matmul_mx(
@@ -149,250 +160,338 @@ def tile_saladsinkhorndustbinaggregation_kernel(tc, h_bytes, h_scale, wp, z, g, 
 
         fgrp, f_codes, f_scales = {}, {}, {}
 
-        def f_group(b, q, half):
-            if half == 0:
-                fgrp[b, q] = sbt("fgrp%d%d" % (b, q), [P, E, PACK], BF16)
-            cols = slice(half * E // 2, (half + 1) * E // 2)
-            nc.scalar.copy(out=fgrp[b, q][:, cols, :], in_=fraw[b, q][:, :, cols].rearrange("p j e -> p e j"))
+        def f_group(b, q, part):
+            if part == 0:
+                fgrp[b, q] = sbt("fgrp%d%d" % (b, q), [P, E, 2, 2], BF16)
+            cols = slice(part * E // 4, (part + 1) * E // 4)
+            nc.scalar.copy(out=fgrp[b, q][:, cols, :, :], in_=fraw[b, q][:, :, cols].rearrange("p (e u) n -> p n u e", u=2))
 
         def f_quant(b, q):
             f_codes[b, q] = sbt("f_codes%d%d" % (b, q), [P, E], U32)
             f_scales[b, q] = sbt("f_scales%d%d" % (b, q), [P, E], U8)
             nc.vector.quantize_mx(
-                out=f_codes[b, q][:].bitcast(FP8X4), scales=f_scales[b, q][:], in_=fgrp[b, q][:].rearrange("p e j -> p (e j)")
+                out=f_codes[b, q][:].bitcast(FP8X4),
+                scales=f_scales[b, q][:],
+                in_=fgrp[b, q][:].rearrange("p n u e -> p (n u e)"),
             )
 
-        def per_batch(name, shape, dtype=F32):
-            return [sbt("%s%d" % (name, b), shape, dtype) for b in range(B)]
-
-        rowmax = per_batch("rowmax", [P, TILES])
+        negt = per_batch("negt", [P, TILES, C + 8])
         negm = per_batch("negm", [P, TILES])
-        rowsum1 = per_batch("rowsum1", [P, TILES])
         zgap = per_batch("zgap", [P, TILES])
-        zgap_min = per_batch("zgap_min", [P, 1])
-        zgap_least = per_batch("zgap_least", [P, 1])
-        ez_row = per_batch("ez_row", [P, TILES])
-        ez_col = per_batch("ez_col", [P, TILES])
-        total1 = per_batch("total1", [P, TILES])
-        u1 = per_batch("u1", [P, TILES])
-        zprod = per_batch("zprod", [P, TILES])
-        zpart = per_batch("zpart", [P, 1])
-        acc = [per_batch("acc_even", [P, C]), per_batch("acc_odd", [P, C])]
-        colmax = per_batch("colmax", [P, CHUNKS])
-        colmax_rows = per_batch("colmax_rows", [P, C])
-        kern = per_batch("kern", [P, TILES, C + PACK])
-        rowsum2 = per_batch("rowsum2", [P, TILES])
-        u2 = per_batch("u2", [P, TILES])
-        junk_s = per_batch("junk_s", [P, TILES, C], BF16)
-        junk_v = per_batch("junk_v", [P, TILES, C + PACK], BF16)
+        junk_a = per_batch("junk_a", [P, TILES, C + PACK], BF16)
+        junk_g = per_batch("junk_g", [P, CHUNKS, S], BF16)
         junk_q = per_batch("junk_q", [P, CHUNKS, E], BF16)
-        shifted = {}
+        junk_r = per_batch("junk_r", [P, TILES, P], BF16)
+        for b in range(B):
+            nc.gpsimd.tensor_copy(out=negt[b][:, :, C], in_=negz[:, b * TILES : (b + 1) * TILES])
+        gate = by_tile("gate", graw, math.sqrt(S))
 
-        def row_max(b, k):
-            nc.vector.tensor_reduce(out=rowmax[b][:, 2 * k : 2 * k + 2], in_=scores[b, k][:], axis=AX.X, op=ALU.max)
-
-        def row_shift(b, q):
-            cols = slice(q * PACK, (q + 1) * PACK)
-            nc.vector.scalar_tensor_tensor(
-                out=negm[b][:, cols],
-                in0=rowmax[b][:, cols],
-                scalar=-1.0,
-                in1=negz[:, b * TILES + q * PACK : b * TILES + (q + 1) * PACK],
+        def row_copy(b, i):
+            nc.vector.tensor_scalar(
+                out=negt[b][:, i, 0:C],
+                in0=scores[b, i // 2][:, i % 2, :],
+                scalar1=-1.0,
+                scalar2=negz[:, b * TILES + i : b * TILES + i + 1],
                 op0=ALU.mult,
                 op1=ALU.min,
+                accum_out=negm[b][:, i : i + 1],
             )
 
-        def row_sum1(b, i):
+        def row_sum(b, i):
             nc.scalar.activation(
-                out=junk_s[b][:, i, :],
-                in_=scores[b, i // 2][:, i % 2, :],
+                out=junk_a[b][:, i, 0 : C + 1],
+                in_=negt[b][:, i, 0 : C + 1],
                 func=ACT.Exp,
+                scale=-1.0,
                 bias=negm[b][:, i : i + 1],
-                accum_out=rowsum1[b][:, i : i + 1],
+                accum_out=total[b][:, i : i + 1],
             )
+
+        total = per_batch("total", [P, TILES])
+        guess = per_batch("guess", [P, TILES])
+        back = per_batch("back", [P, TILES])
+        base = per_batch("base", [P, TILES])
+        ratio = per_batch("ratio", [P, TILES])
+        rest = per_batch("rest", [P, TILES])
+        series = per_batch("series", [P, TILES])
+        lse = per_batch("lse", [P, TILES])
+
+        def log_steps(b):
+            def horner(src, c):
+                return lambda: nc.vector.scalar_tensor_tensor(
+                    out=series[b][:], in0=src[:], scalar=c, in1=rest[b][:], op0=ALU.add, op1=ALU.mult
+                )
+
+            def first_guess():
+                nc.vector.tensor_scalar(
+                    out=guess[b][:],
+                    in0=total[b][:].bitcast(I32),
+                    scalar1=LN2 / 2.0**23,
+                    scalar2=-(127.0 - 0.043) * LN2,
+                    op0=ALU.mult,
+                    op1=ALU.add,
+                )
+                nc.scalar.activation(out=back[b][:], in_=guess[b][:], func=ACT.Exp, scale=-1.0)
+
+            return [
+                first_guess,
+                lambda: nc.vector.tensor_tensor(out=base[b][:], in0=guess[b][:], in1=negm[b][:], op=ALU.subtract),
+                lambda: nc.vector.tensor_tensor(out=ratio[b][:], in0=total[b][:], in1=back[b][:], op=ALU.mult),
+                lambda: nc.vector.tensor_scalar(out=rest[b][:], in0=ratio[b][:], scalar1=-1.0, scalar2=None, op0=ALU.add),
+                horner(rest[b], -6.0 / 5.0),
+                horner(series[b], 6.0 / 4.0),
+                horner(series[b], -6.0 / 3.0),
+                horner(series[b], 6.0 / 2.0),
+                horner(series[b], -6.0),
+                lambda: nc.vector.scalar_tensor_tensor(
+                    out=lse[b][:], in0=series[b][:], scalar=-1.0 / 6.0, in1=base[b][:], op0=ALU.mult, op1=ALU.add
+                ),
+            ]
+
+        gaps = {}
+
+        def turn_scores(b, i):
+            q, pos = divmod(i, PACK)
+            for ch in range(CHUNKS):
+                if pos == 0:
+                    gaps[b, ch, q] = bank(4 * b + 2 * q + ch, "gaps%d%d%d" % (b, ch, q), [P, PACK, P])
+                nc.tensor.matmul(
+                    gaps[b, ch, q][:, pos, :],
+                    lhsT=negt[b][:, i, ch * P : (ch + 1) * P],
+                    rhs=ident[:],
+                    start=(pos == 0),
+                    stop=False,
+                    is_transpose=True,
+                )
+
+        def add_lse(b, ch, q):
+            for pos in range(PACK):
+                i = q * PACK + pos
+                nc.tensor.matmul(
+                    gaps[b, ch, q][:, pos, :],
+                    lhsT=spread(lse[b][:, i : i + 1]),
+                    rhs=ident[:],
+                    start=False,
+                    stop=(pos == PACK - 1),
+                    is_transpose=True,
+                )
+
+        least_part = per_batch("least_part", [P, CHUNKS, PASSES])
+        least = per_batch("least", [P, CHUNKS])
+        kern = per_batch("kern", [P, CHUNKS, S])
+        col_part = [per_batch("col_part%d" % r, [P, CHUNKS, PASSES]) for r in range(2)]
+        col_sum = [per_batch("col_sum%d" % r, [P, CHUNKS]) for r in range(2)]
+        col_inv = [per_batch("col_inv%d" % r, [P, CHUNKS]) for r in range(2)]
+
+        def col_least(b, ch, q):
+            nc.vector.tensor_reduce(
+                out=least_part[b][:, ch, q : q + 1], in_=gaps[b, ch, q][:].rearrange("p a r -> p (a r)"), axis=AX.X, op=ALU.min
+            )
+
+        def col_least_join(b, ch):
+            nc.vector.tensor_tensor(
+                out=least[b][:, ch : ch + 1], in0=least_part[b][:, ch, 0:1], in1=least_part[b][:, ch, 1:2], op=ALU.min
+            )
+
+        def kernel_exp(b, ch, q):
+            nc.scalar.activation(
+                out=kern[b][:, ch, q * SPAN : (q + 1) * SPAN],
+                in_=gaps[b, ch, q][:].rearrange("p a r -> p (a r)"),
+                func=ACT.Exp,
+                scale=-1.0,
+                bias=least[b][:, ch : ch + 1],
+                accum_out=col_part[0][b][:, ch, q : q + 1],
+            )
+
+        def col_join(b, r, ch):
+            nc.vector.tensor_tensor(
+                out=col_sum[r][b][:, ch : ch + 1], in0=col_part[r][b][:, ch, 0:1], in1=col_part[r][b][:, ch, 1:2], op=ALU.add
+            )
+
+        def col_invert(b, r, ch):
+            nc.vector.reciprocal(out=col_inv[r][b][:, ch : ch + 1], in_=col_sum[r][b][:, ch : ch + 1])
+
+        def col_scale(b, ch, q):
+            part = kern[b][:, ch, q * SPAN : (q + 1) * SPAN]
+            nc.scalar.activation(out=part, in_=part, func=ACT.Copy, scale=col_inv[0][b][:, ch : ch + 1])
+
+        def late_bank(b, n):
+            return 4 * b + n
+
+        folded = {}
+
+        def fold(b, ch, q):
+            if ch == 0:
+                folded[b, q] = bank(late_bank(b, q), "folded%d%d" % (b, q), [P, PACK, P])
+            for pos in range(PACK):
+                i = q * PACK + pos
+                nc.tensor.matmul(
+                    folded[b, q][:, pos, :],
+                    lhsT=kern[b][:, ch, i * P : (i + 1) * P],
+                    rhs=ident[:],
+                    start=(ch == 0 and pos == 0),
+                    stop=(ch == CHUNKS - 1 and pos == PACK - 1),
+                    is_transpose=True,
+                )
+
+        zlog = per_batch("zlog", [P, TILES])
+        zlog_min = per_batch("zlog_min", [P, 1])
+        zleast = per_batch("zleast", [P, 1])
+        ez_col = per_batch("ez_col", [P, TILES])
+        zpart = per_batch("zpart", [P, 1])
+        zsum = per_batch("zsum", [P, 1])
+        zinv = per_batch("zinv", [P, 1])
+        dust = per_batch("dust", [P, TILES])
+        zturn = {}
 
         def dust_gap(b):
             nc.gpsimd.tensor_tensor(out=zgap[b][:], in0=negz[:, b * TILES : (b + 1) * TILES], in1=negm[b][:], op=ALU.subtract)
 
-        zturned = {}
+        def dust_min(b, n):
+            nc.vector.tensor_reduce(out=zlog_min[b][:], in_=zgap[b][:], axis=AX.X, op=ALU.min)
+            zturn[b] = bank(n, "zturn_min%d" % b, [P, P])
+            nc.tensor.transpose(zturn[b][:], spread(zlog_min[b][:]), ident[:])
 
-        def dust_min(b):
-            nc.vector.tensor_reduce(out=zgap_min[b][:], in_=zgap[b][:], axis=AX.X, op=ALU.min)
-            zturned[b] = bank("S%d" % b, "zt%d" % b, [P, P])
-            nc.tensor.transpose(zturned[b][:], spread(zgap_min[b][:]), ident[:])
-
-        def dust_shift(b):
-            nc.vector.tensor_reduce(out=zgap_least[b][:], in_=zturned[b][:], axis=AX.X, op=ALU.min)
+        def dust_least(b):
+            nc.vector.tensor_reduce(out=zleast[b][:], in_=zturn[b][:], axis=AX.X, op=ALU.min)
 
         def dust_exp(b):
-            nc.scalar.activation(out=ez_row[b][:], in_=zgap[b][:], func=ACT.Exp, scale=-1.0)
-            nc.scalar.activation(out=ez_col[b][:], in_=zgap[b][:], func=ACT.Exp, scale=-1.0, bias=zgap_least[b][:])
+            nc.gpsimd.tensor_tensor(out=zlog[b][:], in0=negz[:, b * TILES : (b + 1) * TILES], in1=lse[b][:], op=ALU.add)
+            nc.scalar.activation(
+                out=ez_col[b][:], in_=zlog[b][:], func=ACT.Exp, scale=-1.0, bias=zleast[b][:], accum_out=zpart[b][:]
+            )
 
-        def row_total1(b):
-            nc.gpsimd.tensor_tensor(out=total1[b][:], in0=rowsum1[b][:], in1=ez_row[b][:], op=ALU.add)
+        def dust_turn(b, n):
+            zturn[b] = bank(n, "zturn_sum%d" % b, [P, P])
+            nc.tensor.transpose(zturn[b][:], spread(zpart[b][:]), ident[:])
 
-        def col_max_step(b, i):
-            src = scores[b, i // 2][:, i % 2, :]
-            dst = acc[i % 2][b]
-            if i < 2:
-                nc.vector.tensor_scalar(out=dst[:], in0=src, scalar1=negm[b][:, i : i + 1], scalar2=None, op0=ALU.add)
-            else:
-                nc.vector.scalar_tensor_tensor(
-                    out=dst[:], in0=src, scalar=negm[b][:, i : i + 1], in1=dst[:], op0=ALU.add, op1=ALU.max
+        def dust_sum(b):
+            nc.vector.tensor_reduce(out=zsum[b][:], in_=zturn[b][:], axis=AX.X, op=ALU.add)
+
+        def dust_invert(b):
+            nc.vector.reciprocal(out=zinv[b][:], in_=zsum[b][:])
+            nc.gpsimd.tensor_scalar(
+                out=dust[b][:], in0=ez_col[b][:], scalar1=zinv[b][:], scalar2=float(S - C) / 1.0, op0=ALU.mult, op1=ALU.mult
+            )
+
+        row2 = per_batch("row2", [P, TILES])
+        total2 = per_batch("total2", [P, TILES])
+        row_inv = per_batch("row_inv", [P, TILES])
+        weight = per_batch("weight", [P, TILES])
+
+        def row2_sum(b, q):
+            nc.vector.tensor_reduce(out=row2[b][:, q * PACK : (q + 1) * PACK], in_=folded[b, q][:], axis=AX.X, op=ALU.add)
+
+        def row2_total(b, q):
+            cols = slice(q * PACK, (q + 1) * PACK)
+            nc.vector.tensor_tensor(out=total2[b][:, cols], in0=row2[b][:, cols], in1=dust[b][:, cols], op=ALU.add)
+
+        def row2_scalar(b, q):
+            for pos in range(PACK):
+                i = q * PACK + pos
+                nc.scalar.activation(
+                    out=junk_r[b][:, i, :],
+                    in_=folded[b, q][:, pos, :],
+                    func=ACT.Identity,
+                    bias=dust[b][:, i : i + 1],
+                    accum_out=total2[b][:, i : i + 1],
                 )
 
-        acc_turned = {}
+        inv_rows, weight_rows = {}, {}
 
-        def col_max_turn(b, par):
-            if par == 0:
-                acc_turned[b] = bank("S%d" % b, "acc_turned%d" % b, [P, CHUNKS, 2, P])
-            for ch in range(CHUNKS):
-                nc.tensor.transpose(acc_turned[b][:, ch, par, :], acc[par][b][:, ch * P : (ch + 1) * P], ident[:])
-
-        def col_max_finish(b):
-            nc.vector.tensor_reduce(
-                out=colmax[b][:], in_=acc_turned[b][:].rearrange("p c a r -> p c (a r)"), axis=AX.X, op=ALU.max
-            )
-            rows = spread_columns(b, "colmax_ps%d" % b, [colmax[b][:, ch : ch + 1] for ch in range(CHUNKS)])
-            nc.scalar.copy(out=colmax_rows[b][:], in_=rows[:])
-
-        def spread_columns(b, name, cols):
-            rows = bank("S%d" % b, name, [P, len(cols) * P])
-            for ch in range(len(cols)):
-                nc.tensor.transpose(rows[:, ch * P : (ch + 1) * P], spread(cols[ch]), ident[:])
+        def spread_tokens(n, name, src, q):
+            rows = bank(n, name, [P, SPAN])
+            for pos in range(PACK):
+                i = q * PACK + pos
+                nc.tensor.transpose(rows[:, pos * P : (pos + 1) * P], spread(src[:, i : i + 1]), ident[:])
             return rows
 
-        def row_weights1(b):
-            nc.vector.reciprocal(out=u1[b][:], in_=total1[b][:])
+        def row2_invert(b, q):
+            cols = slice(q * PACK, (q + 1) * PACK)
+            nc.vector.reciprocal(out=row_inv[b][:, cols], in_=total2[b][:, cols])
+            inv_rows[b, q] = spread_tokens(late_bank(b, 2 + q), "inv_rows%d%d" % (b, q), row_inv[b], q)
 
-        def dust_partial(b):
+        def gate_weight(b, q):
+            cols = slice(q * PACK, (q + 1) * PACK)
+            nc.gpsimd.tensor_tensor(
+                out=weight[b][:, cols], in0=row_inv[b][:, cols], in1=gate[:, b * TILES + q * PACK : b * TILES + (q + 1) * PACK], op=ALU.mult
+            )
+
+        def weight_turn(b, q):
+            weight_rows[b, q] = spread_tokens(late_bank(b, q), "weight_rows%d%d" % (b, q), weight[b], q)
+
+        def col2_sum(b, ch, q):
+            cols = slice(q * SPAN, (q + 1) * SPAN)
             nc.vector.scalar_tensor_tensor(
-                out=zprod[b][:], in0=ez_col[b][:], scalar=1.0, in1=u1[b][:], op0=ALU.mult, op1=ALU.mult, accum_out=zpart[b][:]
-            )
-            nc.scalar.activation(out=kern[b][:, :, C], in_=zprod[b][:], func=ACT.Copy, scale=float(S - C))
-
-        def col_shift(b, k):
-            shifted[b, k] = sbt("shifted%d%d" % (b, k), [P, 2, C], F32)
-            nc.vector.tensor_tensor(
-                out=shifted[b, k][:],
-                in0=scores[b, k][:],
-                in1=colmax_rows[b][:].unsqueeze(1).to_broadcast([P, 2, C]),
-                op=ALU.subtract,
-            )
-
-        def kernel_exp(b, i):
-            nc.scalar.activation(
-                out=kern[b][:, i, 0:C], in_=shifted[b, i // 2][:, i % 2, :], func=ACT.Exp, bias=negm[b][:, i : i + 1]
-            )
-
-        sums = {}
-
-        def scale_rows_by(b, r, i, on_scalar):
-            weights = u1[b] if r == 1 else u2[b]
-            tile = kern[b][:, i, 0:C]
-            if on_scalar:
-                nc.scalar.activation(out=tile, in_=tile, func=ACT.Copy, scale=weights[:, i : i + 1])
-            else:
-                nc.vector.tensor_scalar(out=tile, in0=tile, scalar1=weights[:, i : i + 1], scalar2=None, op0=ALU.mult)
-
-        def col_sum_open(b, r):
-            sums[b, r] = [bank("H%d" % ch, "colsum%d%d%d" % (b, r, ch), [P, 2, P]) for ch in range(CHUNKS)]
-            if r == 1:
-                nc.tensor.transpose(sums[b, r][0][:, 0, :], spread(zpart[b][:]), ident[:])
-
-        def col_sum_step(b, r, i):
-            for ch in range(CHUNKS):
-                nc.tensor.matmul(
-                    sums[b, r][ch][:, 1, :],
-                    lhsT=kern[b][:, i, ch * P : (ch + 1) * P],
-                    rhs=ident[:],
-                    start=(i == 0),
-                    stop=(i == TILES - 1),
-                    is_transpose=True,
-                )
-
-        vrows, csum, vcol = {}, {}, {}
-
-        def col_total(b, r):
-            first = 0 if r == 1 else 1
-            csum[b, r] = sbt("csum%d%d" % (b, r), [P, 3], F32)
-            nc.vector.tensor_reduce(out=csum[b, r][:, first:2], in_=sums[b, r][0][:, first:2, :], axis=AX.X, op=ALU.add)
-            nc.vector.tensor_reduce(out=csum[b, r][:, 2:3], in_=sums[b, r][1][:, 1:2, :], axis=AX.X, op=ALU.add)
-
-        def col_weights(b, r):
-            first = 0 if r == 1 else 1
-            vcol = sbt("vcol%d%d" % (b, r), [P, 3], F32)
-            nc.vector.reciprocal(out=vcol[:, first:3], in_=csum[b, r][:, first:3])
-            cols = [vcol[:, 1:2], vcol[:, 2:3]] + ([vcol[:, 0:1]] if r == 1 else [])
-            vrows[b, r] = spread_columns(b, "vrows%d%d" % (b, r), cols)
-
-        def row_sum2(b, i):
-            nc.vector.scalar_tensor_tensor(
-                out=junk_v[b][:, i, 0 : C + 1],
-                in0=kern[b][:, i, 0 : C + 1],
+                out=junk_g[b][:, ch, cols],
+                in0=kern[b][:, ch, cols],
                 scalar=1.0,
-                in1=vrows[b, 1][:, 0 : C + 1],
+                in1=inv_rows[b, q][:],
                 op0=ALU.mult,
                 op1=ALU.mult,
-                accum_out=rowsum2[b][:, i : i + 1],
+                accum_out=col_part[1][b][:, ch, q : q + 1],
             )
 
-        def row_weights2(b, lo, hi):
-            nc.vector.reciprocal(out=u2[b][:, lo:hi], in_=rowsum2[b][:, lo:hi])
+        pg, pturn, pgrp, p_mx = {}, {}, {}, {}
 
-        pg, pgrp, p_codes, p_scales = {}, {}, {}, {}
-
-        def assign(b, i):
-            q, j = divmod(i, PACK)
-            if j == 0:
-                pg[b, q] = sbt("pg%d%d" % (b, q), [P, PACK, C], BF16)
+        def assign(b, ch, q):
+            pg[b, ch, q] = sbt("pg%d%d%d" % (b, ch, q), [P, SPAN], BF16)
             nc.vector.scalar_tensor_tensor(
-                out=pg[b, q][:, j, :],
-                in0=kern[b][:, i, 0:C],
-                scalar=gate[:, b * TILES + i : b * TILES + i + 1],
-                in1=vrows[b, 2][:],
+                out=pg[b, ch, q][:],
+                in0=kern[b][:, ch, q * SPAN : (q + 1) * SPAN],
+                scalar=col_inv[1][b][:, ch : ch + 1],
+                in1=weight_rows[b, q][:],
                 op0=ALU.mult,
                 op1=ALU.mult,
             )
 
-        def p_group(b, q, on_scalar):
-            pgrp[b, q] = sbt("pgrp%d%d" % (b, q), [P, C, PACK], BF16)
-            if on_scalar:
-                nc.scalar.copy(out=pgrp[b, q][:], in_=pg[b, q][:].rearrange("p j c -> p c j"))
-            else:
-                nc.vector.tensor_copy(out=pgrp[b, q][:], in_=pg[b, q][:].rearrange("p j c -> p c j"))
+        def p_turn(b, ch, q):
+            pturn[b, ch, q] = bank(late_bank(b, 2 + q), "pturn%d%d%d" % (b, ch, q), [P, 2, P])
+            words = pg[b, ch, q][:].bitcast(F32)
+            for u in range(2):
+                nc.tensor.transpose(pturn[b, ch, q][:, u, :], words[:, u * P : (u + 1) * P], ident[:])
 
-        def p_quant(b, q):
-            p_codes[b, q] = sbt("p_codes%d%d" % (b, q), [P, C], U32)
-            p_scales[b, q] = sbt("p_scales%d%d" % (b, q), [P, C], U8)
-            nc.vector.quantize_mx(
-                out=p_codes[b, q][:].bitcast(FP8X4), scales=p_scales[b, q][:], in_=pgrp[b, q][:].rearrange("p c j -> p (c j)")
+        def p_group(b, ch, q):
+            pgrp[b, ch, q] = sbt("pgrp%d%d%d" % (b, ch, q), [P, SPAN], BF16)
+            nc.scalar.copy(
+                out=pgrp[b, ch, q][:].bitcast(F32).rearrange("p (r u) -> p r u", u=2), in_=pturn[b, ch, q][:].rearrange("p u r -> p r u")
             )
 
         agg = {}
 
-        def aggregate(b, q):
-            for ch in range(CHUNKS):
-                if q == 0:
-                    agg[b, ch] = bank("T%d" % (CHUNKS * b + ch), "agg%d%d" % (b, ch), [P, E])
-                cols = slice(ch * P, (ch + 1) * P)
-                nc.tensor.matmul_mx(
-                    out=agg[b, ch][:],
-                    lhsT=p_codes[b, q][:, cols].bitcast(FP8X4),
-                    lhsT_scale=p_scales[b, q][:, cols],
-                    rhs=f_codes[b, q][:].bitcast(FP8X4),
-                    rhs_scale=f_scales[b, q][:],
-                    start=(q == 0),
-                    stop=(q == PASSES - 1),
-                )
+        def p_quant(b, ch, q):
+            codes = sbt("p_codes%d%d%d" % (b, ch, q), [P, P], U32)
+            scales = sbt("p_scales%d%d%d" % (b, ch, q), [P, P], U8)
+            nc.vector.quantize_mx(out=codes[:].bitcast(FP8X4), scales=scales[:], in_=pgrp[b, ch, q][:])
+            p_mx[b, ch, q] = (codes, scales)
 
-        root, inv = {}, {}
+        def aggregate(b, ch, q):
+            codes, scales = p_mx[b, ch, q]
+            if q == 0:
+                agg[b, ch] = bank(CHUNKS * b + ch, "agg%d%d" % (b, ch), [P, E])
+            nc.tensor.matmul_mx(
+                out=agg[b, ch][:],
+                lhsT=codes[:].bitcast(FP8X4),
+                lhsT_scale=scales[:],
+                rhs=f_codes[b, q][:].bitcast(FP8X4),
+                rhs_scale=f_scales[b, q][:],
+                start=(q == 0),
+                stop=(q == PASSES - 1),
+            )
+
+        sq, root, inv = {}, {}, {}
+
+        def preload_root_table():
+            warm = sbt("warm", [P, 1], F32)
+            nc.scalar.activation(out=warm[:], in_=col_inv[0][B - 1][:, 0:1], func=ACT.Sqrt)
+
+        def norm_square(b, ch):
+            sq[b, ch] = sbt("sq%d%d" % (b, ch), [P, 1], F32)
+            nc.scalar.activation(out=junk_q[b][:, ch, :], in_=agg[b, ch][:], func=ACT.Square, accum_out=sq[b, ch][:])
 
         def norm_root(b, ch):
-            sq = sbt("sq%d%d" % (b, ch), [P, 1], F32)
             root[b, ch] = sbt("root%d%d" % (b, ch), [P, 1], F32)
-            nc.scalar.activation(out=junk_q[b][:, ch, :], in_=agg[b, ch][:], func=ACT.Square, accum_out=sq[:])
-            nc.scalar.activation(out=root[b, ch][:], in_=sq[:], func=ACT.Sqrt, scale=1.0 / E, bias=1e-6)
+            nc.scalar.activation(out=root[b, ch][:], in_=sq[b, ch][:], func=ACT.Sqrt, scale=1.0 / E, bias=1e-6)
 
         def norm_inverse(b, ch):
             inv[b, ch] = sbt("inv%d%d" % (b, ch), [P, 1], F32)
@@ -406,176 +505,278 @@ def tile_saladsinkhorndustbinaggregation_kernel(tc, h_bytes, h_scale, wp, z, g, 
                 nc.vector.tensor_scalar(out=y[:], in0=agg[b, ch][:], scalar1=inv[b, ch][:], scalar2=None, op0=ALU.mult)
             nc.sync.dma_start(out=out[b, ch * P : (ch + 1) * P, :], in_=y[:])
 
-        ctx.enter_context(tc.manual_schedule())
+        def weave(first, second):
+            for n in range(max(len(first), len(second))):
+                for steps in (first, second):
+                    if n < len(steps):
+                        steps[n]()
+
+        def step(fn, *args):
+            return lambda: fn(*args)
+
+        def chain(*steps):
+            return lambda: [s() for s in steps]
+
+
+        def copy_pair(b, k):
+            row_copy(b, 2 * k)
+            row_copy(b, 2 * k + 1)
+
+        def sum_pair(b, k):
+            row_sum(b, 2 * k)
+            row_sum(b, 2 * k + 1)
+
+        def widen_pair(b, k):
+            h_widen(b, 2 * k)
+            h_widen(b, 2 * k + 1)
+            h_turn(b, k)
+            h_group(b, k)
+
+        def quant_pair(b, k):
+            h_quant(b, k)
+            score_matmul(b, k)
+
+        def turn_half(b, q):
+            for i in range(q * PACK, (q + 1) * PACK):
+                turn_scores(b, i)
+
+        def add_chunk(b, ch):
+            for q in range(PASSES):
+                add_lse(b, ch, q)
+
+        def exp_chunk(b, ch):
+            col_least_join(b, ch)
+            for q in range(PASSES):
+                kernel_exp(b, ch, q)
+
+        def scale_chunk(b, ch):
+            for q in range(PASSES):
+                col_scale(b, ch, q)
+
+        def rows2(b, q):
+            if False:
+                row2_scalar(b, q)
+            else:
+                row2_sum(b, q)
+
+        def total_rows2(b, q):
+            if not False:
+                row2_total(b, q)
+
+        def invert_rows2(b, q):
+            row2_invert(b, q)
+            gate_weight(b, q)
+
+        def p_move(b, ch, q):
+            p_turn(b, ch, q)
+            p_group(b, ch, q)
+
+        def p_pass(b, ch, q):
+            p_quant(b, ch, q)
+            aggregate(b, ch, q)
+
+        def f_parts(b, q, lo, hi):
+            for part in range(lo, hi):
+                f_group(b, q, part)
 
         w_group()
-        for k in range(PAIRS):
-            h_widen(0, 2 * k)
-            if k == 1:
-                w_quant()
-            if k > 1:
-                h_quant(0, k - 2)
-                score_matmul(0, k - 2)
-            h_widen(0, 2 * k + 1)
-            h_turn(0, k)
-            if k > 1:
-                f_group(0, 0, k - 2)
+        widen_pair(0, 0)
+        f_parts(0, 0, 0, 1)
+        w_quant()
+        widen_pair(0, 1)
+        f_parts(0, 0, 1, 2)
+        h_widen(0, 4)
+        quant_pair(0, 0)
+        h_widen(0, 5)
+        h_turn(0, 2)
+        h_group(0, 2)
+        quant_pair(0, 1)
+        copy_pair(0, 0)
+        sum_pair(0, 0)
+        f_parts(0, 0, 2, 3)
+        widen_pair(0, 3)
+        quant_pair(0, 2)
+        copy_pair(0, 1)
+        sum_pair(0, 1)
+        f_parts(0, 0, 3, 4)
         h_widen(1, 0)
-        h_quant(0, 2)
-        score_matmul(0, 2)
-        row_max(0, 0)
-        h_quant(0, 3)
-        score_matmul(0, 3)
-        row_max(0, 1)
+        quant_pair(0, 3)
+        turn_half(0, 0)
+        copy_pair(0, 2)
+        sum_pair(0, 2)
         h_widen(1, 1)
         h_turn(1, 0)
-        f_group(0, 1, 0)
-        row_shift(0, 0)
-        row_max(0, 2)
-        row_max(0, 3)
-        h_widen(1, 2)
-        row_shift(0, 1)
+        copy_pair(0, 3)
+        sum_pair(0, 3)
         dust_gap(0)
-        for i in range(TILES):
-            col_max_step(0, i)
-            row_sum1(0, (i + 2) % TILES)
-            if i == 2:
-                dust_min(0)
-            if i == 5:
-                dust_shift(0)
-            if i >= TILES - 2:
-                col_max_turn(0, i % 2)
-        dust_exp(0)
-        row_total1(0)
+        h_group(1, 0)
+        turn_half(0, 1)
+        h_widen(1, 2)
         h_widen(1, 3)
         h_turn(1, 1)
+        log0 = log_steps(0)
+        log0[0]()
+        f_parts(0, 1, 0, 1)
+        h_group(1, 1)
+        quant_pair(1, 0)
+        log0[1]()
         h_widen(1, 4)
-        col_max_finish(0)
-        h_widen(1, 5)
-        h_turn(1, 2)
-        row_weights1(0)
-        h_widen(1, 6)
-        dust_partial(0)
-        h_widen(1, 7)
-        h_turn(1, 3)
-        f_group(0, 1, 1)
-        h_quant(1, 0)
-        col_sum_open(0, 1)
-        for k in range(PAIRS):
-            col_shift(0, k)
-            if k < PAIRS - 1:
-                h_quant(1, k + 1)
-            score_matmul(1, k)
-            kernel_exp(0, 2 * k)
-            kernel_exp(0, 2 * k + 1)
-            if True:
-                for i in (2 * k, 2 * k + 1):
-                    scale_rows_by(0, 1, i, True)
-                    col_sum_step(0, 1, i)
-        for k in range(PAIRS):
-            row_max(1, k)
-            if k == 2:
-                row_shift(1, 0)
-            if not True:
-                for i in (2 * k, 2 * k + 1):
-                    scale_rows_by(0, 1, i, False)
-                    col_sum_step(0, 1, i)
-        f_quant(0, 0)
-        row_shift(1, 1)
+        f_parts(0, 1, 1, 2)
+        weave(log0[2:], [
+            chain(step(h_widen, 1, 5), step(h_turn, 1, 2), step(h_group, 1, 2), step(f_parts, 0, 1, 2, 3)),
+            step(quant_pair, 1, 1),
+            chain(step(h_widen, 1, 6)),
+            chain(step(h_widen, 1, 7), step(h_turn, 1, 3)),
+            chain(step(row_copy, 1, 0)),
+            chain(step(row_copy, 1, 1), step(h_group, 1, 3), step(sum_pair, 1, 0)),
+            step(quant_pair, 1, 2),
+            ])
+        add_chunk(0, 0)
+        copy_pair(1, 1)
+        sum_pair(1, 1)
+        f_parts(0, 1, 3, 4)
+        quant_pair(1, 3)
+        add_chunk(0, 1)
+        copy_pair(1, 2)
+        sum_pair(1, 2)
+        col_least(0, 0, 0)
+        copy_pair(1, 3)
+        sum_pair(1, 3)
         dust_gap(1)
-        for i in range(TILES):
-            col_max_step(1, i)
-            row_sum1(1, (i + 2) % TILES)
-            if i == 1:
-                col_total(0, 1)
-            if i == 2:
-                dust_min(1)
-            if i == 3:
-                col_weights(0, 1)
-            if i == 5:
-                dust_shift(1)
-            if i >= TILES - 2:
-                col_max_turn(1, i % 2)
-        dust_exp(1)
-        row_total1(1)
-        f_group(1, 0, 0)
-        col_sum_open(0, 2)
-        for i in range(TILES):
-            row_sum2(0, i)
-            if i == 2:
-                col_max_finish(1)
-            if i == PACK:
-                row_weights2(0, 0, PACK)
-                for ii in range(PACK):
-                    scale_rows_by(0, 2, ii, True)
-                    col_sum_step(0, 2, ii)
-            if i == 5:
-                row_weights1(1)
-        dust_partial(1)
-        row_weights2(0, PACK, TILES)
-        for ii in range(PACK, TILES):
-            scale_rows_by(0, 2, ii, True)
-            col_sum_step(0, 2, ii)
-        for k in range(PAIRS):
-            col_shift(1, k)
-            kernel_exp(1, 2 * k)
-            kernel_exp(1, 2 * k + 1)
-            if k == 2:
-                col_total(0, 2)
-        col_weights(0, 2)
+        dust_min(0, 6)
+        col_least(0, 0, 1)
+        log1 = log_steps(1)
+        log1[0]()
+        exp_chunk(0, 0)
+        dust_least(0)
+        dust_exp(0)
+        turn_half(1, 0)
+        turn_half(1, 1)
+        log1[1]()
+        col_least(0, 1, 0)
+        log1[2]()
+        col_least(0, 1, 1)
+        log1[3]()
+        col_join(0, 0, 0)
+        exp_chunk(0, 1)
+        log1[4]()
+        col_invert(0, 0, 0)
+        scale_chunk(0, 0)
+        dust_turn(0, 0)
+        log1[5]()
+        f_quant(0, 0)
+        log1[6]()
+        dust_sum(0)
+        log1[7]()
+        col_join(0, 0, 1)
+        log1[8]()
+        col_invert(0, 0, 1)
+        scale_chunk(0, 1)
+        f_parts(1, 0, 0, 3)
+        log1[9]()
+        dust_invert(0)
         f_quant(0, 1)
-        col_sum_open(1, 1)
-        for i in range(TILES):
-            scale_rows_by(1, 1, i, True)
-            col_sum_step(1, 1, i)
-        for i in range(TILES):
-            assign(0, i)
-            if i == PACK - 1:
-                p_group(0, 0, True)
-            if i == 5:
-                col_total(1, 1)
-        col_weights(1, 1)
-        p_group(0, 1, True)
-        f_group(1, 0, 1)
-        p_quant(0, 0)
-        aggregate(0, 0)
-        col_sum_open(1, 2)
-        for i in range(TILES):
-            row_sum2(1, i)
-            if i == 2:
-                p_quant(0, 1)
-                aggregate(0, 1)
-            if i == PACK:
-                row_weights2(1, 0, PACK)
-                for ii in range(PACK):
-                    scale_rows_by(1, 2, ii, True)
-                    col_sum_step(1, 2, ii)
-        row_weights2(1, PACK, TILES)
-        for ii in range(PACK, TILES):
-            scale_rows_by(1, 2, ii, True)
-            col_sum_step(1, 2, ii)
-        f_quant(1, 0)
-        f_group(1, 1, 0)
-        f_group(1, 1, 1)
-        col_total(1, 2)
-        col_weights(1, 2)
+        fold(0, 0, 0)
+        add_chunk(1, 0)
+        dust_min(1, 3)
+        fold(0, 1, 0)
+        add_chunk(1, 1)
+        fold(0, 0, 1)
+        fold(0, 1, 1)
+        col_least(1, 0, 0)
+        dust_least(1)
+        dust_exp(1)
+        col_least(1, 0, 1)
+        rows2(0, 0)
+        exp_chunk(1, 0)
+        col_least(1, 1, 0)
+        total_rows2(0, 0)
+        col_least(1, 1, 1)
+        invert_rows2(0, 0)
+        exp_chunk(1, 1)
+        rows2(0, 1)
+        col_join(1, 0, 0)
+        total_rows2(0, 1)
+        col_invert(1, 0, 0)
+        scale_chunk(1, 0)
+        invert_rows2(0, 1)
+        dust_turn(1, 4)
+        col2_sum(0, 0, 0)
+        col_join(1, 0, 1)
+        col2_sum(0, 1, 0)
+        col_invert(1, 0, 1)
+        scale_chunk(1, 1)
+        f_parts(1, 0, 3, 4)
+        f_parts(1, 1, 0, 4)
+        preload_root_table()
+        dust_sum(1)
+        fold(1, 0, 0)
+        weight_turn(0, 0)
+        col2_sum(0, 0, 1)
+        dust_invert(1)
+        fold(1, 1, 0)
+        weight_turn(0, 1)
+        col2_sum(0, 1, 1)
+        col_join(0, 1, 0)
+        col_join(0, 1, 1)
+        fold(1, 0, 1)
+        fold(1, 1, 1)
+        rows2(1, 0)
+        col_invert(0, 1, 0)
+        col_invert(0, 1, 1)
+        total_rows2(1, 0)
+        assign(0, 0, 0)
+        invert_rows2(1, 0)
+        rows2(1, 1)
+        assign(0, 0, 1)
+        total_rows2(1, 1)
+        p_move(0, 0, 0)
+        assign(0, 1, 0)
+        invert_rows2(1, 1)
+        p_move(0, 0, 1)
+        assign(0, 1, 1)
+        p_move(0, 1, 0)
+        p_move(0, 1, 1)
+        col2_sum(1, 0, 0)
+        p_pass(0, 0, 0)
+        weight_turn(1, 0)
+        col2_sum(1, 0, 1)
+        p_pass(0, 0, 1)
+        weight_turn(1, 1)
+        col2_sum(1, 1, 0)
+        col_join(1, 1, 0)
+        p_pass(0, 1, 0)
+        col2_sum(1, 1, 1)
+        col_invert(1, 1, 0)
+        p_pass(0, 1, 1)
+        col_join(1, 1, 1)
+        norm_square(0, 0)
         norm_root(0, 0)
+        assign(1, 0, 0)
+        col_invert(1, 1, 1)
+        p_move(1, 0, 0)
+        assign(1, 0, 1)
+        norm_inverse(0, 0)
+        norm_square(0, 1)
+        p_move(1, 0, 1)
         norm_root(0, 1)
+        assign(1, 1, 0)
+        f_quant(1, 0)
+        p_move(1, 1, 0)
+        p_pass(1, 0, 0)
+        assign(1, 1, 1)
         f_quant(1, 1)
-        for i in range(TILES):
-            assign(1, i)
-            if i == PACK - 1:
-                p_group(1, 0, True)
-        p_group(1, 1, False)
-        p_quant(1, 0)
-        aggregate(1, 0)
-        p_quant(1, 1)
-        aggregate(1, 1)
-        for ch in range(CHUNKS):
-            norm_inverse(0, ch)
-            store(0, ch, False)
-        for ch in range(CHUNKS):
-            norm_root(1, ch)
+        p_move(1, 1, 1)
+        p_pass(1, 0, 1)
+        p_pass(1, 1, 0)
+        norm_inverse(0, 1)
+        p_pass(1, 1, 1)
+        store(0, 0, False)
+        norm_square(1, 0)
+        norm_root(1, 0)
+        store(0, 1, False)
+        norm_square(1, 1)
+        norm_root(1, 1)
         for ch in range(CHUNKS):
             norm_inverse(1, ch)
-            store(1, ch, ch == 0)
+            store(1, ch, False)

@@ -68,16 +68,18 @@ def tile_saladsinkhorndustbinaggregation_kernel(tc, h_bytes, h_scale, wp, z, g, 
         nc.sync.dma_start(out=wraw[:], in_=wp.rearrange("(p j) c -> p j c", j=PACK))
         load_h(0, 0)
         load_h(0, 1)
-        zraw = sbt("zraw", [P, B * PASSES * 2, 2], BF16)
-        nc.sync.dma_start(out=zraw[:], in_=z.rearrange("b (a p j) -> p (b a) j", p=P, j=2))
+        zrows = sbt("zrows", [P, P], F32)
+        nc.vector.memset(zrows[:], 0.0)
+        nc.sync.dma_start(out=zrows[0 : B * PAIRS, :].bitcast(BF16), in_=z.rearrange("b (a n) -> (b a) n", n=2 * P))
         load_f(0, 0)
         load_f(0, 1)
         load_h(1, 0)
         load_h(1, 1)
         load_f(1, 0)
         load_f(1, 1)
-        graw = sbt("graw", [P, B * PASSES * 2, 2], BF16)
-        nc.sync.dma_start(out=graw[:], in_=g.rearrange("b (a p j) -> p (b a) j", p=P, j=2))
+        gate_rows = per_batch("gate_rows", [P, S], BF16)
+        for b in range(B):
+            nc.sync.dma_start(out=gate_rows[b][:], in_=g[b].partition_broadcast(P))
 
         ident = sbt("ident", [P, P], F32)
         make_identity(nc, ident[:])
@@ -92,19 +94,15 @@ def tile_saladsinkhorndustbinaggregation_kernel(tc, h_bytes, h_scale, wp, z, g, 
             func=ACT.Copy,
         )
 
-        def by_tile(name, raw, factor):
-            dst = sbt(name, [P, B * TILES], F32)
-            nc.gpsimd.tensor_scalar(
-                out=dst[:].rearrange("p (q j a) -> p q j a", j=2, a=2),
-                in0=raw[:].rearrange("p (q a) j -> p q j a", a=2),
-                scalar1=factor,
-                scalar2=0.0,
-                op0=ALU.mult,
-                op1=ALU.add,
-            )
-            return dst
-
-        negz = by_tile("negz", zraw, -1.0)
+        z_ps = bank(0, "z_ps", [P, P])
+        nc.tensor.transpose(z_ps[:], zrows[:], ident[:])
+        negz = sbt("negz", [P, B * TILES], F32)
+        nc.scalar.activation(
+            out=negz[:].rearrange("p (q j a) -> p q j a", j=2, a=2),
+            in_=z_ps[:, 0 : B * PAIRS].bitcast(BF16).rearrange("p (q a j) -> p q j a", j=2, a=2),
+            func=ACT.Copy,
+            scale=-1.0,
+        )
 
         w_codes = sbt("w_codes", [P, C], U32)
         w_scales = sbt("w_scales", [P, C], U8)
@@ -164,7 +162,10 @@ def tile_saladsinkhorndustbinaggregation_kernel(tc, h_bytes, h_scale, wp, z, g, 
             if part == 0:
                 fgrp[b, q] = sbt("fgrp%d%d" % (b, q), [P, E, 2, 2], BF16)
             cols = slice(part * E // 4, (part + 1) * E // 4)
-            nc.scalar.copy(out=fgrp[b, q][:, cols, :, :], in_=fraw[b, q][:, :, cols].rearrange("p (e u) n -> p n u e", u=2))
+            nc.scalar.copy(
+                out=fgrp[b, q][:, cols, :, :].rearrange("p (c i) u e -> p c u e i", i=PACK),
+                in_=fraw[b, q][:, :, cols].rearrange("p (e u) (c i) -> p c u e i", u=2, i=PACK),
+            )
 
         def f_quant(b, q):
             f_codes[b, q] = sbt("f_codes%d%d" % (b, q), [P, E], U32)
@@ -179,12 +180,10 @@ def tile_saladsinkhorndustbinaggregation_kernel(tc, h_bytes, h_scale, wp, z, g, 
         negm = per_batch("negm", [P, TILES])
         zgap = per_batch("zgap", [P, TILES])
         junk_a = per_batch("junk_a", [P, TILES, C + PACK], BF16)
-        junk_g = per_batch("junk_g", [P, CHUNKS, S], BF16)
         junk_q = per_batch("junk_q", [P, CHUNKS, E], BF16)
         junk_r = per_batch("junk_r", [P, TILES, P], BF16)
         for b in range(B):
             nc.gpsimd.tensor_copy(out=negt[b][:, :, C], in_=negz[:, b * TILES : (b + 1) * TILES])
-        gate = by_tile("gate", graw, math.sqrt(S))
 
         def row_copy(b, i):
             nc.vector.tensor_scalar(
@@ -304,8 +303,13 @@ def tile_saladsinkhorndustbinaggregation_kernel(tc, h_bytes, h_scale, wp, z, g, 
             )
 
         def col_join(b, r, ch):
-            nc.vector.tensor_tensor(
-                out=col_sum[r][b][:, ch : ch + 1], in0=col_part[r][b][:, ch, 0:1], in1=col_part[r][b][:, ch, 1:2], op=ALU.add
+            nc.vector.tensor_scalar(
+                out=col_sum[r][b][:, ch : ch + 1],
+                in0=col_part[r][b][:, ch, 0:1],
+                scalar1=col_part[r][b][:, ch, 1:2],
+                scalar2=1.0 if r == 0 else 1.0 / math.sqrt(S),
+                op0=ALU.add,
+                op1=ALU.mult,
             )
 
         def col_invert(b, r, ch):
@@ -345,7 +349,7 @@ def tile_saladsinkhorndustbinaggregation_kernel(tc, h_bytes, h_scale, wp, z, g, 
         zturn = {}
 
         def dust_gap(b):
-            nc.gpsimd.tensor_tensor(out=zgap[b][:], in0=negz[:, b * TILES : (b + 1) * TILES], in1=negm[b][:], op=ALU.subtract)
+            nc.vector.tensor_tensor(out=zgap[b][:], in0=negz[:, b * TILES : (b + 1) * TILES], in1=negm[b][:], op=ALU.subtract)
 
         def dust_min(b, n):
             nc.vector.tensor_reduce(out=zlog_min[b][:], in_=zgap[b][:], axis=AX.X, op=ALU.min)
@@ -355,8 +359,10 @@ def tile_saladsinkhorndustbinaggregation_kernel(tc, h_bytes, h_scale, wp, z, g, 
         def dust_least(b):
             nc.vector.tensor_reduce(out=zleast[b][:], in_=zturn[b][:], axis=AX.X, op=ALU.min)
 
+        def dust_log(b):
+            nc.vector.tensor_tensor(out=zlog[b][:], in0=negz[:, b * TILES : (b + 1) * TILES], in1=lse[b][:], op=ALU.add)
+
         def dust_exp(b):
-            nc.gpsimd.tensor_tensor(out=zlog[b][:], in0=negz[:, b * TILES : (b + 1) * TILES], in1=lse[b][:], op=ALU.add)
             nc.scalar.activation(
                 out=ez_col[b][:], in_=zlog[b][:], func=ACT.Exp, scale=-1.0, bias=zleast[b][:], accum_out=zpart[b][:]
             )
@@ -370,14 +376,15 @@ def tile_saladsinkhorndustbinaggregation_kernel(tc, h_bytes, h_scale, wp, z, g, 
 
         def dust_invert(b):
             nc.vector.reciprocal(out=zinv[b][:], in_=zsum[b][:])
-            nc.gpsimd.tensor_scalar(
-                out=dust[b][:], in0=ez_col[b][:], scalar1=zinv[b][:], scalar2=float(S - C) / 1.0, op0=ALU.mult, op1=ALU.mult
+
+        def dust_scale(b):
+            nc.vector.tensor_scalar(
+                out=dust[b][:], in0=ez_col[b][:], scalar1=zinv[b][:], scalar2=float(S - C) / (P if b == 1 else 1.0), op0=ALU.mult, op1=ALU.mult
             )
 
         row2 = per_batch("row2", [P, TILES])
         total2 = per_batch("total2", [P, TILES])
         row_inv = per_batch("row_inv", [P, TILES])
-        weight = per_batch("weight", [P, TILES])
 
         def row2_sum(b, q):
             nc.vector.tensor_reduce(out=row2[b][:, q * PACK : (q + 1) * PACK], in_=folded[b, q][:], axis=AX.X, op=ALU.add)
@@ -397,7 +404,7 @@ def tile_saladsinkhorndustbinaggregation_kernel(tc, h_bytes, h_scale, wp, z, g, 
                     accum_out=total2[b][:, i : i + 1],
                 )
 
-        inv_rows, weight_rows = {}, {}
+        inv_rows = {}
 
         def spread_tokens(n, name, src, q):
             rows = bank(n, name, [P, SPAN])
@@ -411,19 +418,10 @@ def tile_saladsinkhorndustbinaggregation_kernel(tc, h_bytes, h_scale, wp, z, g, 
             nc.vector.reciprocal(out=row_inv[b][:, cols], in_=total2[b][:, cols])
             inv_rows[b, q] = spread_tokens(late_bank(b, 2 + q), "inv_rows%d%d" % (b, q), row_inv[b], q)
 
-        def gate_weight(b, q):
-            cols = slice(q * PACK, (q + 1) * PACK)
-            nc.gpsimd.tensor_tensor(
-                out=weight[b][:, cols], in0=row_inv[b][:, cols], in1=gate[:, b * TILES + q * PACK : b * TILES + (q + 1) * PACK], op=ALU.mult
-            )
-
-        def weight_turn(b, q):
-            weight_rows[b, q] = spread_tokens(late_bank(b, q), "weight_rows%d%d" % (b, q), weight[b], q)
-
         def col2_sum(b, ch, q):
             cols = slice(q * SPAN, (q + 1) * SPAN)
             nc.vector.scalar_tensor_tensor(
-                out=junk_g[b][:, ch, cols],
+                out=kern[b][:, ch, cols],
                 in0=kern[b][:, ch, cols],
                 scalar=1.0,
                 in1=inv_rows[b, q][:],
@@ -437,16 +435,16 @@ def tile_saladsinkhorndustbinaggregation_kernel(tc, h_bytes, h_scale, wp, z, g, 
         def assign(b, ch, q):
             pg[b, ch, q] = sbt("pg%d%d%d" % (b, ch, q), [P, SPAN], BF16)
             nc.vector.scalar_tensor_tensor(
-                out=pg[b, ch, q][:],
-                in0=kern[b][:, ch, q * SPAN : (q + 1) * SPAN],
+                out=pg[b, ch, q][:].rearrange("p (j r) -> p j r", j=2),
+                in0=kern[b][:, ch, q * SPAN : (q + 1) * SPAN].rearrange("p (j r) -> p j r", j=2),
                 scalar=col_inv[1][b][:, ch : ch + 1],
-                in1=weight_rows[b, q][:],
+                in1=gate_rows[b][:, q * SPAN : (q + 1) * SPAN].rearrange("p (r j) -> p j r", j=2),
                 op0=ALU.mult,
                 op1=ALU.mult,
             )
 
         def p_turn(b, ch, q):
-            pturn[b, ch, q] = bank(late_bank(b, 2 + q), "pturn%d%d%d" % (b, ch, q), [P, 2, P])
+            pturn[b, ch, q] = bank(late_bank(b, q), "pturn%d%d%d" % (b, ch, q), [P, 2, P])
             words = pg[b, ch, q][:].bitcast(F32)
             for u in range(2):
                 nc.tensor.transpose(pturn[b, ch, q][:, u, :], words[:, u * P : (u + 1) * P], ident[:])
@@ -468,7 +466,7 @@ def tile_saladsinkhorndustbinaggregation_kernel(tc, h_bytes, h_scale, wp, z, g, 
         def aggregate(b, ch, q):
             codes, scales = p_mx[b, ch, q]
             if q == 0:
-                agg[b, ch] = bank(CHUNKS * b + ch, "agg%d%d" % (b, ch), [P, E])
+                agg[b, ch] = bank(late_bank(b, 2 + ch), "agg%d%d" % (b, ch), [P, E])
             nc.tensor.matmul_mx(
                 out=agg[b, ch][:],
                 lhsT=codes[:].bitcast(FP8X4),
@@ -483,7 +481,7 @@ def tile_saladsinkhorndustbinaggregation_kernel(tc, h_bytes, h_scale, wp, z, g, 
 
         def preload_root_table():
             warm = sbt("warm", [P, 1], F32)
-            nc.scalar.activation(out=warm[:], in_=col_inv[0][B - 1][:, 0:1], func=ACT.Sqrt)
+            nc.scalar.activation(out=warm[:], in_=col_inv[0][B - 1][:, 0:1], func=ACT.Abs_reciprocal_sqrt)
 
         def norm_square(b, ch):
             sq[b, ch] = sbt("sq%d%d" % (b, ch), [P, 1], F32)
@@ -491,19 +489,21 @@ def tile_saladsinkhorndustbinaggregation_kernel(tc, h_bytes, h_scale, wp, z, g, 
 
         def norm_root(b, ch):
             root[b, ch] = sbt("root%d%d" % (b, ch), [P, 1], F32)
-            nc.scalar.activation(out=root[b, ch][:], in_=sq[b, ch][:], func=ACT.Sqrt, scale=1.0 / E, bias=1e-6)
+            nc.scalar.activation(out=root[b, ch][:], in_=sq[b, ch][:], func=ACT.Abs_reciprocal_sqrt, scale=1.0 / E, bias=1e-6)
 
         def norm_inverse(b, ch):
             inv[b, ch] = sbt("inv%d%d" % (b, ch), [P, 1], F32)
-            nc.vector.reciprocal(out=inv[b, ch][:], in_=root[b, ch][:])
+            nc.vector.reciprocal(out=root[b, ch][:], in_=root[b, ch][:])
 
-        def store(b, ch, on_scalar):
-            y = sbt("y%d%d" % (b, ch), [P, E], F32)
-            if on_scalar:
-                nc.scalar.activation(out=y[:], in_=agg[b, ch][:], func=ACT.Copy, scale=inv[b, ch][:])
-            else:
-                nc.vector.tensor_scalar(out=y[:], in0=agg[b, ch][:], scalar1=inv[b, ch][:], scalar2=None, op0=ALU.mult)
-            nc.sync.dma_start(out=out[b, ch * P : (ch + 1) * P, :], in_=y[:])
+        def store(b, ch, parts, on_scalar=False):
+            for part in range(parts):
+                cols = slice(part * E // parts, (part + 1) * E // parts)
+                y = sbt("y%d%d%d" % (b, ch, part), [P, E // parts], F32)
+                if on_scalar:
+                    nc.scalar.activation(out=y[:], in_=agg[b, ch][:, cols], func=ACT.Copy, scale=root[b, ch][:])
+                else:
+                    nc.vector.tensor_scalar(out=y[:], in0=agg[b, ch][:, cols], scalar1=root[b, ch][:], scalar2=None, op0=ALU.mult)
+                nc.sync.dma_start(out=out[b, ch * P : (ch + 1) * P, cols], in_=y[:])
 
         def weave(first, second):
             for n in range(max(len(first), len(second))):
@@ -554,18 +554,17 @@ def tile_saladsinkhorndustbinaggregation_kernel(tc, h_bytes, h_scale, wp, z, g, 
                 col_scale(b, ch, q)
 
         def rows2(b, q):
-            if False:
+            if b == 1:
                 row2_scalar(b, q)
             else:
                 row2_sum(b, q)
 
         def total_rows2(b, q):
-            if not False:
+            if b == 0:
                 row2_total(b, q)
 
         def invert_rows2(b, q):
             row2_invert(b, q)
-            gate_weight(b, q)
 
         def p_move(b, ch, q):
             p_turn(b, ch, q)
@@ -575,16 +574,19 @@ def tile_saladsinkhorndustbinaggregation_kernel(tc, h_bytes, h_scale, wp, z, g, 
             p_quant(b, ch, q)
             aggregate(b, ch, q)
 
-        def f_parts(b, q, lo, hi):
-            for part in range(lo, hi):
-                f_group(b, q, part)
+        f_todo = [(b, q, part) for b in reversed(range(B)) for q in reversed(range(PASSES)) for part in reversed(range(4))]
+
+        def f_parts(n):
+            for k in range(n):
+                f_group(*f_todo[-1])
+                f_todo.remove(f_todo[-1])
 
         w_group()
         widen_pair(0, 0)
-        f_parts(0, 0, 0, 1)
+        f_parts(1)
         w_quant()
         widen_pair(0, 1)
-        f_parts(0, 0, 1, 2)
+        f_parts(2)
         h_widen(0, 4)
         quant_pair(0, 0)
         h_widen(0, 5)
@@ -593,12 +595,12 @@ def tile_saladsinkhorndustbinaggregation_kernel(tc, h_bytes, h_scale, wp, z, g, 
         quant_pair(0, 1)
         copy_pair(0, 0)
         sum_pair(0, 0)
-        f_parts(0, 0, 2, 3)
+        f_parts(1)
         widen_pair(0, 3)
         quant_pair(0, 2)
         copy_pair(0, 1)
         sum_pair(0, 1)
-        f_parts(0, 0, 3, 4)
+        f_parts(1)
         h_widen(1, 0)
         quant_pair(0, 3)
         turn_half(0, 0)
@@ -608,22 +610,22 @@ def tile_saladsinkhorndustbinaggregation_kernel(tc, h_bytes, h_scale, wp, z, g, 
         h_turn(1, 0)
         copy_pair(0, 3)
         sum_pair(0, 3)
-        dust_gap(0)
         h_group(1, 0)
         turn_half(0, 1)
         h_widen(1, 2)
+        dust_gap(0)
         h_widen(1, 3)
         h_turn(1, 1)
         log0 = log_steps(0)
         log0[0]()
-        f_parts(0, 1, 0, 1)
+        f_parts(1)
         h_group(1, 1)
         quant_pair(1, 0)
         log0[1]()
         h_widen(1, 4)
-        f_parts(0, 1, 1, 2)
+        f_parts(1)
         weave(log0[2:], [
-            chain(step(h_widen, 1, 5), step(h_turn, 1, 2), step(h_group, 1, 2), step(f_parts, 0, 1, 2, 3)),
+            chain(step(h_widen, 1, 5), step(h_turn, 1, 2), step(h_group, 1, 2), step(f_parts, 2)),
             step(quant_pair, 1, 1),
             chain(step(h_widen, 1, 6)),
             chain(step(h_widen, 1, 7), step(h_turn, 1, 3)),
@@ -631,152 +633,152 @@ def tile_saladsinkhorndustbinaggregation_kernel(tc, h_bytes, h_scale, wp, z, g, 
             chain(step(row_copy, 1, 1), step(h_group, 1, 3), step(sum_pair, 1, 0)),
             step(quant_pair, 1, 2),
             ])
-        add_chunk(0, 0)
         copy_pair(1, 1)
         sum_pair(1, 1)
-        f_parts(0, 1, 3, 4)
+        f_parts(1)
         quant_pair(1, 3)
-        add_chunk(0, 1)
+        add_chunk(0, 0)
         copy_pair(1, 2)
+        dust_log(0)
         sum_pair(1, 2)
-        col_least(0, 0, 0)
         copy_pair(1, 3)
         sum_pair(1, 3)
-        dust_gap(1)
+        add_chunk(0, 1)
         dust_min(0, 6)
-        col_least(0, 0, 1)
+        col_least(0, 0, 0)
+        dust_gap(1)
         log1 = log_steps(1)
         log1[0]()
-        exp_chunk(0, 0)
-        dust_least(0)
-        dust_exp(0)
+        f_parts(1)
+        log1[1]()
+        col_least(0, 0, 1)
+        log1[2]()
         turn_half(1, 0)
         turn_half(1, 1)
-        log1[1]()
-        col_least(0, 1, 0)
-        log1[2]()
-        col_least(0, 1, 1)
+        exp_chunk(0, 0)
         log1[3]()
+        dust_least(0)
+        dust_exp(0)
+        log1[4]()
+        col_least(0, 1, 0)
+        log1[5]()
+        col_least(0, 1, 1)
+        log1[6]()
         col_join(0, 0, 0)
         exp_chunk(0, 1)
-        log1[4]()
+        log1[7]()
         col_invert(0, 0, 0)
         scale_chunk(0, 0)
         dust_turn(0, 0)
-        log1[5]()
-        f_quant(0, 0)
-        log1[6]()
-        dust_sum(0)
-        log1[7]()
-        col_join(0, 0, 1)
         log1[8]()
+        dust_sum(0)
+        log1[9]()
+        add_chunk(1, 0)
+        f_quant(0, 0)
+        col_join(0, 0, 1)
+        dust_invert(0)
+        dust_log(1)
         col_invert(0, 0, 1)
         scale_chunk(0, 1)
-        f_parts(1, 0, 0, 3)
-        log1[9]()
-        dust_invert(0)
-        f_quant(0, 1)
+        f_parts(1)
+        dust_scale(0)
         fold(0, 0, 0)
-        add_chunk(1, 0)
-        dust_min(1, 3)
-        fold(0, 1, 0)
         add_chunk(1, 1)
+        fold(0, 1, 0)
+        dust_min(1, 3)
         fold(0, 0, 1)
         fold(0, 1, 1)
         col_least(1, 0, 0)
-        dust_least(1)
-        dust_exp(1)
         col_least(1, 0, 1)
-        rows2(0, 0)
+        f_quant(0, 1)
         exp_chunk(1, 0)
         col_least(1, 1, 0)
-        total_rows2(0, 0)
         col_least(1, 1, 1)
-        invert_rows2(0, 0)
+        rows2(0, 0)
         exp_chunk(1, 1)
+        dust_least(1)
+        dust_exp(1)
+        total_rows2(0, 0)
         rows2(0, 1)
+        invert_rows2(0, 0)
         col_join(1, 0, 0)
         total_rows2(0, 1)
         col_invert(1, 0, 0)
         scale_chunk(1, 0)
         invert_rows2(0, 1)
-        dust_turn(1, 4)
-        col2_sum(0, 0, 0)
         col_join(1, 0, 1)
-        col2_sum(0, 1, 0)
+        dust_turn(1, 4)
+        f_quant(1, 0)
         col_invert(1, 0, 1)
         scale_chunk(1, 1)
-        f_parts(1, 0, 3, 4)
-        f_parts(1, 1, 0, 4)
-        preload_root_table()
+        f_parts(2)
+        col2_sum(0, 0, 0)
         dust_sum(1)
         fold(1, 0, 0)
-        weight_turn(0, 0)
         col2_sum(0, 0, 1)
         dust_invert(1)
         fold(1, 1, 0)
-        weight_turn(0, 1)
-        col2_sum(0, 1, 1)
+        col2_sum(0, 1, 0)
+        dust_scale(1)
         col_join(0, 1, 0)
-        col_join(0, 1, 1)
         fold(1, 0, 1)
         fold(1, 1, 1)
         rows2(1, 0)
-        col_invert(0, 1, 0)
-        col_invert(0, 1, 1)
-        total_rows2(1, 0)
-        assign(0, 0, 0)
-        invert_rows2(1, 0)
         rows2(1, 1)
+        f_parts(2)
+        col2_sum(0, 1, 1)
+        col_invert(0, 1, 0)
+        col_join(0, 1, 1)
+        assign(0, 0, 0)
+        col_invert(0, 1, 1)
+        p_turn(0, 0, 0)
         assign(0, 0, 1)
-        total_rows2(1, 1)
-        p_move(0, 0, 0)
+        invert_rows2(1, 0)
+        p_turn(0, 0, 1)
+        p_group(0, 0, 0)
+        p_group(0, 0, 1)
         assign(0, 1, 0)
         invert_rows2(1, 1)
-        p_move(0, 0, 1)
         assign(0, 1, 1)
         p_move(0, 1, 0)
         p_move(0, 1, 1)
+        preload_root_table()
         col2_sum(1, 0, 0)
+        f_quant(1, 1)
         p_pass(0, 0, 0)
-        weight_turn(1, 0)
-        col2_sum(1, 0, 1)
         p_pass(0, 0, 1)
-        weight_turn(1, 1)
-        col2_sum(1, 1, 0)
-        col_join(1, 1, 0)
+        col2_sum(1, 0, 1)
         p_pass(0, 1, 0)
-        col2_sum(1, 1, 1)
+        col_join(1, 1, 0)
+        col2_sum(1, 1, 0)
         col_invert(1, 1, 0)
         p_pass(0, 1, 1)
-        col_join(1, 1, 1)
         norm_square(0, 0)
+        col2_sum(1, 1, 1)
         norm_root(0, 0)
-        assign(1, 0, 0)
-        col_invert(1, 1, 1)
-        p_move(1, 0, 0)
-        assign(1, 0, 1)
-        norm_inverse(0, 0)
         norm_square(0, 1)
-        p_move(1, 0, 1)
+        assign(1, 0, 0)
+        col_join(1, 1, 1)
+        p_move(1, 0, 0)
         norm_root(0, 1)
+        assign(1, 0, 1)
+        col_invert(1, 1, 1)
+        p_move(1, 0, 1)
+        store(0, 0, 1, True)
         assign(1, 1, 0)
-        f_quant(1, 0)
+        p_quant(1, 0, 0)
         p_move(1, 1, 0)
-        p_pass(1, 0, 0)
+        aggregate(1, 0, 0)
         assign(1, 1, 1)
-        f_quant(1, 1)
+        p_quant(1, 0, 1)
         p_move(1, 1, 1)
-        p_pass(1, 0, 1)
+        aggregate(1, 0, 1)
         p_pass(1, 1, 0)
-        norm_inverse(0, 1)
         p_pass(1, 1, 1)
-        store(0, 0, False)
         norm_square(1, 0)
+        store(0, 1, 1)
         norm_root(1, 0)
-        store(0, 1, False)
         norm_square(1, 1)
+        store(1, 0, 1)
         norm_root(1, 1)
-        for ch in range(CHUNKS):
-            norm_inverse(1, ch)
-            store(1, ch, False)
+        store(1, 1, 2)

@@ -25,7 +25,10 @@ PASSES = S // SPAN
 TILES = PASSES * PACK
 PAIRS = TILES // 2
 CHUNKS = C // P
+ROW = C + 8
+F_PARTS = 4
 LN2 = math.log(2.0)
+LOG2_MIDDLE = 0.043
 
 
 def tile_saladsinkhorndustbinaggregation_kernel(tc, h_bytes, h_scale, wp, z, g, f, out):
@@ -38,17 +41,18 @@ def tile_saladsinkhorndustbinaggregation_kernel(tc, h_bytes, h_scale, wp, z, g, 
         def sbt(name, shape, dtype):
             return sb.tile(shape, dtype, name=name, tag=name, align_bytes=64)
 
+        def per_batch(name, shape, dtype=F32):
+            return [sbt("%s%d" % (name, b), shape, dtype) for b in range(B)]
+
         def bank(n, name, shape):
             return ps.tile(shape, F32, name=name, tag="bank%d" % n)
+
+        def own_bank(b, n):
+            return 4 * b + n
 
         def spread(col):
             return col.to_broadcast([P, P])
 
-        def per_batch(name, shape, dtype=F32):
-            return [sbt("%s%d" % (name, b), shape, dtype) for b in range(B)]
-
-        hs = sbt("hs", [P, PACK], F32)
-        nc.sync.dma_start(out=hs[:], in_=h_scale.rearrange("a o (p t) -> p (a o t)", t=PACK))
         hbytes, fraw = {}, {}
 
         def load_h(b, q):
@@ -64,13 +68,15 @@ def tile_saladsinkhorndustbinaggregation_kernel(tc, h_bytes, h_scale, wp, z, g, 
                 out=fraw[b, q][:], in_=f[b, q * SPAN : (q + 1) * SPAN, :].rearrange("(p j) e -> p j e", j=PACK)
             )
 
+        hs = sbt("hs", [P, PACK], F32)
+        nc.sync.dma_start(out=hs[:], in_=h_scale.rearrange("a o (p t) -> p (a o t)", t=PACK))
         wraw = sbt("wraw", [P, PACK, C], BF16)
         nc.sync.dma_start(out=wraw[:], in_=wp.rearrange("(p j) c -> p j c", j=PACK))
         load_h(0, 0)
-        load_h(0, 1)
         zrows = sbt("zrows", [P, P], F32)
         nc.vector.memset(zrows[:], 0.0)
         nc.sync.dma_start(out=zrows[0 : B * PAIRS, :].bitcast(BF16), in_=z.rearrange("b (a n) -> (b a) n", n=2 * P))
+        load_h(0, 1)
         load_f(0, 0)
         load_f(0, 1)
         load_h(1, 0)
@@ -103,18 +109,39 @@ def tile_saladsinkhorndustbinaggregation_kernel(tc, h_bytes, h_scale, wp, z, g, 
             func=ACT.Copy,
             scale=-1.0,
         )
+        negt = per_batch("negt", [P, TILES, ROW])
+        for b in range(B):
+            nc.gpsimd.tensor_copy(out=negt[b][:, :, C], in_=negz[:, b * TILES : (b + 1) * TILES])
 
-        w_codes = sbt("w_codes", [P, C], U32)
-        w_scales = sbt("w_scales", [P, C], U8)
+        def quantize(name, src, words):
+            codes = sbt(name + "_codes", [P, words], U32)
+            scales = sbt(name + "_scales", [P, words], U8)
+            nc.vector.quantize_mx(out=codes[:].bitcast(FP8X4), scales=scales[:], in_=src)
+            return codes, scales
+
+        def matmul_mx(dst, lhs, lhs_cols, rhs, start, stop):
+            nc.tensor.matmul_mx(
+                out=dst,
+                lhsT=lhs[0][:, lhs_cols].bitcast(FP8X4),
+                lhsT_scale=lhs[1][:, lhs_cols],
+                rhs=rhs[0][:].bitcast(FP8X4),
+                rhs_scale=rhs[1][:],
+                start=start,
+                stop=stop,
+            )
+
+        def add_turned(dst, src, start, stop):
+            nc.tensor.matmul(dst, lhsT=src, rhs=ident[:], start=start, stop=stop, is_transpose=True)
+
+        mx = {}
+        hwide, hturn, hgrp, scores = {}, {}, {}, {}
         wgrp = sbt("wgrp", [P, C, PACK], BF16)
 
         def w_group():
             nc.vector.tensor_copy(out=wgrp[:], in_=wraw[:].rearrange("p j c -> p c j"))
 
         def w_quant():
-            nc.vector.quantize_mx(out=w_codes[:].bitcast(FP8X4), scales=w_scales[:], in_=wgrp[:].rearrange("p c j -> p (c j)"))
-
-        hwide, hturn, hgrp, h_codes, h_scales, scores = {}, {}, {}, {}, {}, {}
+            mx["w"] = quantize("w", wgrp[:].rearrange("p c j -> p (c j)"), C)
 
         def h_widen(b, i):
             q, j, a = i // PACK, (i // 2) % 2, i % 2
@@ -124,11 +151,11 @@ def tile_saladsinkhorndustbinaggregation_kernel(tc, h_bytes, h_scale, wp, z, g, 
             )
 
         def h_turn(b, k):
-            hturn[b, k] = bank(4 + k % 2, "turned%d%d" % (b, k), [P, 2, 2, P])
-            for jj in range(2):
-                words = hwide[b, 2 * k + jj][:].bitcast(F32)
+            hturn[b, k] = bank(4 + k % 2, "hturn%d%d" % (b, k), [P, 2, 2, P])
+            for a in range(2):
+                words = hwide[b, 2 * k + a][:].bitcast(F32)
                 for u in range(2):
-                    nc.tensor.transpose(hturn[b, k][:, jj, u, :], words[:, u : H // 2 : 2], ident[:])
+                    nc.tensor.transpose(hturn[b, k][:, a, u, :], words[:, u : H // 2 : 2], ident[:])
 
         def h_group(b, k):
             hgrp[b, k] = sbt("hgrp%d%d" % (b, k), [P, 2 * SPAN], BF16)
@@ -137,53 +164,32 @@ def tile_saladsinkhorndustbinaggregation_kernel(tc, h_bytes, h_scale, wp, z, g, 
                 in_=hturn[b, k][:].rearrange("p a u r -> p a r u"),
             )
 
-        def h_quant(b, k):
-            h_codes[b, k] = sbt("h_codes%d%d" % (b, k), [P, 2 * P], U32)
-            h_scales[b, k] = sbt("h_scales%d%d" % (b, k), [P, 2 * P], U8)
-            nc.vector.quantize_mx(out=h_codes[b, k][:].bitcast(FP8X4), scales=h_scales[b, k][:], in_=hgrp[b, k][:])
-
-        def score_matmul(b, k):
+        def score_pair(b, k):
+            h_mx = quantize("h%d%d" % (b, k), hgrp[b, k][:], 2 * P)
             scores[b, k] = bank(6 + k % 2, "scores%d%d" % (b, k), [P, 2, C])
-            for jj in range(2):
-                cols = slice(jj * P, (jj + 1) * P)
-                nc.tensor.matmul_mx(
-                    out=scores[b, k][:, jj, :],
-                    lhsT=h_codes[b, k][:, cols].bitcast(FP8X4),
-                    lhsT_scale=h_scales[b, k][:, cols],
-                    rhs=w_codes[:].bitcast(FP8X4),
-                    rhs_scale=w_scales[:],
-                    start=True,
-                    stop=True,
+            for a in range(2):
+                matmul_mx(scores[b, k][:, a, :], h_mx, slice(a * P, (a + 1) * P), mx["w"], True, True)
+
+        fgrp = {}
+        f_todo = [(b, q, part) for b in range(B) for q in range(PASSES) for part in range(F_PARTS)]
+
+        def f_parts(count, copy):
+            for b, q, part in f_todo[0:count]:
+                if part == 0:
+                    fgrp[b, q] = sbt("fgrp%d%d" % (b, q), [P, E, 2, 2], BF16)
+                cols = slice(part * E // F_PARTS, (part + 1) * E // F_PARTS)
+                copy(
+                    out=fgrp[b, q][:, cols, :, :].rearrange("p (c i) u e -> p c u e i", i=PACK),
+                    in_=fraw[b, q][:, :, cols].rearrange("p (e u) (c i) -> p c u e i", u=2, i=PACK),
                 )
-
-        fgrp, f_codes, f_scales = {}, {}, {}
-
-        def f_group(b, q, part):
-            if part == 0:
-                fgrp[b, q] = sbt("fgrp%d%d" % (b, q), [P, E, 2, 2], BF16)
-            cols = slice(part * E // 4, (part + 1) * E // 4)
-            nc.scalar.copy(
-                out=fgrp[b, q][:, cols, :, :].rearrange("p (c i) u e -> p c u e i", i=PACK),
-                in_=fraw[b, q][:, :, cols].rearrange("p (e u) (c i) -> p c u e i", u=2, i=PACK),
-            )
+                f_todo.remove((b, q, part))
 
         def f_quant(b, q):
-            f_codes[b, q] = sbt("f_codes%d%d" % (b, q), [P, E], U32)
-            f_scales[b, q] = sbt("f_scales%d%d" % (b, q), [P, E], U8)
-            nc.vector.quantize_mx(
-                out=f_codes[b, q][:].bitcast(FP8X4),
-                scales=f_scales[b, q][:],
-                in_=fgrp[b, q][:].rearrange("p n u e -> p (n u e)"),
-            )
+            mx["f", b, q] = quantize("f%d%d" % (b, q), fgrp[b, q][:].rearrange("p n u e -> p (n u e)"), E)
 
-        negt = per_batch("negt", [P, TILES, C + 8])
         negm = per_batch("negm", [P, TILES])
-        zgap = per_batch("zgap", [P, TILES])
-        junk_a = per_batch("junk_a", [P, TILES, C + PACK], BF16)
-        junk_q = per_batch("junk_q", [P, CHUNKS, E], BF16)
-        junk_r = per_batch("junk_r", [P, TILES, P], BF16)
-        for b in range(B):
-            nc.gpsimd.tensor_copy(out=negt[b][:, :, C], in_=negz[:, b * TILES : (b + 1) * TILES])
+        total = per_batch("total", [P, TILES])
+        spent_exp = per_batch("spent_exp", [P, TILES, ROW], BF16)
 
         def row_copy(b, i):
             nc.vector.tensor_scalar(
@@ -196,17 +202,17 @@ def tile_saladsinkhorndustbinaggregation_kernel(tc, h_bytes, h_scale, wp, z, g, 
                 accum_out=negm[b][:, i : i + 1],
             )
 
-        def row_sum(b, i):
-            nc.scalar.activation(
-                out=junk_a[b][:, i, 0 : C + 1],
-                in_=negt[b][:, i, 0 : C + 1],
-                func=ACT.Exp,
-                scale=-1.0,
-                bias=negm[b][:, i : i + 1],
-                accum_out=total[b][:, i : i + 1],
-            )
+        def row_sums(b, k):
+            for i in (2 * k, 2 * k + 1):
+                nc.scalar.activation(
+                    out=spent_exp[b][:, i, 0 : C + 1],
+                    in_=negt[b][:, i, 0 : C + 1],
+                    func=ACT.Exp,
+                    scale=-1.0,
+                    bias=negm[b][:, i : i + 1],
+                    accum_out=total[b][:, i : i + 1],
+                )
 
-        total = per_batch("total", [P, TILES])
         guess = per_batch("guess", [P, TILES])
         back = per_batch("back", [P, TILES])
         base = per_batch("base", [P, TILES])
@@ -216,21 +222,21 @@ def tile_saladsinkhorndustbinaggregation_kernel(tc, h_bytes, h_scale, wp, z, g, 
         lse = per_batch("lse", [P, TILES])
 
         def log_steps(b):
-            def horner(src, c):
-                return lambda: nc.vector.scalar_tensor_tensor(
-                    out=series[b][:], in0=src[:], scalar=c, in1=rest[b][:], op0=ALU.add, op1=ALU.mult
-                )
-
             def first_guess():
                 nc.vector.tensor_scalar(
                     out=guess[b][:],
                     in0=total[b][:].bitcast(I32),
                     scalar1=LN2 / 2.0**23,
-                    scalar2=-(127.0 - 0.043) * LN2,
+                    scalar2=-(127.0 - LOG2_MIDDLE) * LN2,
                     op0=ALU.mult,
                     op1=ALU.add,
                 )
                 nc.scalar.activation(out=back[b][:], in_=guess[b][:], func=ACT.Exp, scale=-1.0)
+
+            def horner(src, c):
+                return lambda: nc.vector.scalar_tensor_tensor(
+                    out=series[b][:], in0=src[:], scalar=c, in1=rest[b][:], op0=ALU.add, op1=ALU.mult
+                )
 
             return [
                 first_guess,
@@ -247,60 +253,55 @@ def tile_saladsinkhorndustbinaggregation_kernel(tc, h_bytes, h_scale, wp, z, g, 
                 ),
             ]
 
+        riders = []
+
+        def ride():
+            for rider in riders[0:1]:
+                rider()
+                riders.remove(rider)
+
         gaps = {}
 
         def turn_scores(b, i):
             q, pos = divmod(i, PACK)
             for ch in range(CHUNKS):
                 if pos == 0:
-                    gaps[b, ch, q] = bank(4 * b + 2 * q + ch, "gaps%d%d%d" % (b, ch, q), [P, PACK, P])
-                nc.tensor.matmul(
-                    gaps[b, ch, q][:, pos, :],
-                    lhsT=negt[b][:, i, ch * P : (ch + 1) * P],
-                    rhs=ident[:],
-                    start=(pos == 0),
-                    stop=False,
-                    is_transpose=True,
-                )
+                    gaps[b, ch, q] = bank(own_bank(b, CHUNKS * q + ch), "gaps%d%d%d" % (b, ch, q), [P, PACK, P])
+                add_turned(gaps[b, ch, q][:, pos, :], negt[b][:, i, ch * P : (ch + 1) * P], pos == 0, False)
 
         def add_lse(b, ch, q):
             for pos in range(PACK):
                 i = q * PACK + pos
-                nc.tensor.matmul(
-                    gaps[b, ch, q][:, pos, :],
-                    lhsT=spread(lse[b][:, i : i + 1]),
-                    rhs=ident[:],
-                    start=False,
-                    stop=(pos == PACK - 1),
-                    is_transpose=True,
-                )
+                add_turned(gaps[b, ch, q][:, pos, :], spread(lse[b][:, i : i + 1]), False, pos == PACK - 1)
 
         least_part = per_batch("least_part", [P, CHUNKS, PASSES])
         least = per_batch("least", [P, CHUNKS])
-        kern = per_batch("kern", [P, CHUNKS, S])
+        plan = per_batch("plan", [P, CHUNKS, S])
         col_part = [per_batch("col_part%d" % r, [P, CHUNKS, PASSES]) for r in range(2)]
         col_sum = [per_batch("col_sum%d" % r, [P, CHUNKS]) for r in range(2)]
         col_inv = [per_batch("col_inv%d" % r, [P, CHUNKS]) for r in range(2)]
+
+        def pass_cols(q):
+            return slice(q * SPAN, (q + 1) * SPAN)
 
         def col_least(b, ch, q):
             nc.vector.tensor_reduce(
                 out=least_part[b][:, ch, q : q + 1], in_=gaps[b, ch, q][:].rearrange("p a r -> p (a r)"), axis=AX.X, op=ALU.min
             )
 
-        def col_least_join(b, ch):
+        def col_exp(b, ch):
             nc.vector.tensor_tensor(
                 out=least[b][:, ch : ch + 1], in0=least_part[b][:, ch, 0:1], in1=least_part[b][:, ch, 1:2], op=ALU.min
             )
-
-        def kernel_exp(b, ch, q):
-            nc.scalar.activation(
-                out=kern[b][:, ch, q * SPAN : (q + 1) * SPAN],
-                in_=gaps[b, ch, q][:].rearrange("p a r -> p (a r)"),
-                func=ACT.Exp,
-                scale=-1.0,
-                bias=least[b][:, ch : ch + 1],
-                accum_out=col_part[0][b][:, ch, q : q + 1],
-            )
+            for q in range(PASSES):
+                nc.scalar.activation(
+                    out=plan[b][:, ch, pass_cols(q)],
+                    in_=gaps[b, ch, q][:].rearrange("p a r -> p (a r)"),
+                    func=ACT.Exp,
+                    scale=-1.0,
+                    bias=least[b][:, ch : ch + 1],
+                    accum_out=col_part[0][b][:, ch, q : q + 1],
+                )
 
         def col_join(b, r, ch):
             nc.vector.tensor_scalar(
@@ -315,33 +316,15 @@ def tile_saladsinkhorndustbinaggregation_kernel(tc, h_bytes, h_scale, wp, z, g, 
         def col_invert(b, r, ch):
             nc.vector.reciprocal(out=col_inv[r][b][:, ch : ch + 1], in_=col_sum[r][b][:, ch : ch + 1])
 
-        def col_scale(b, ch, q):
-            part = kern[b][:, ch, q * SPAN : (q + 1) * SPAN]
-            nc.scalar.activation(out=part, in_=part, func=ACT.Copy, scale=col_inv[0][b][:, ch : ch + 1])
+        def col_scale(b, ch):
+            for q in range(PASSES):
+                part = plan[b][:, ch, pass_cols(q)]
+                nc.scalar.activation(out=part, in_=part, func=ACT.Copy, scale=col_inv[0][b][:, ch : ch + 1])
 
-        def late_bank(b, n):
-            return 4 * b + n
-
-        folded = {}
-
-        def fold(b, ch, q):
-            if ch == 0:
-                folded[b, q] = bank(late_bank(b, q), "folded%d%d" % (b, q), [P, PACK, P])
-            for pos in range(PACK):
-                i = q * PACK + pos
-                nc.tensor.matmul(
-                    folded[b, q][:, pos, :],
-                    lhsT=kern[b][:, ch, i * P : (i + 1) * P],
-                    rhs=ident[:],
-                    start=(ch == 0 and pos == 0),
-                    stop=(ch == CHUNKS - 1 and pos == PACK - 1),
-                    is_transpose=True,
-                )
-
-        zlog = per_batch("zlog", [P, TILES])
-        zlog_min = per_batch("zlog_min", [P, 1])
+        zgap = per_batch("zgap", [P, TILES])
+        zgap_min = per_batch("zgap_min", [P, 1])
         zleast = per_batch("zleast", [P, 1])
-        ez_col = per_batch("ez_col", [P, TILES])
+        zexp = per_batch("zexp", [P, TILES])
         zpart = per_batch("zpart", [P, 1])
         zsum = per_batch("zsum", [P, 1])
         zinv = per_batch("zinv", [P, 1])
@@ -349,26 +332,21 @@ def tile_saladsinkhorndustbinaggregation_kernel(tc, h_bytes, h_scale, wp, z, g, 
         zturn = {}
 
         def dust_gap(b):
-            nc.vector.tensor_tensor(out=zgap[b][:], in0=negz[:, b * TILES : (b + 1) * TILES], in1=negm[b][:], op=ALU.subtract)
+            nc.vector.tensor_tensor(out=zgap[b][:], in0=negz[:, b * TILES : (b + 1) * TILES], in1=lse[b][:], op=ALU.add)
 
-        def dust_min(b, n):
-            nc.vector.tensor_reduce(out=zlog_min[b][:], in_=zgap[b][:], axis=AX.X, op=ALU.min)
-            zturn[b] = bank(n, "zturn_min%d" % b, [P, P])
-            nc.tensor.transpose(zturn[b][:], spread(zlog_min[b][:]), ident[:])
-
-        def dust_least(b):
-            nc.vector.tensor_reduce(out=zleast[b][:], in_=zturn[b][:], axis=AX.X, op=ALU.min)
-
-        def dust_log(b):
-            nc.vector.tensor_tensor(out=zlog[b][:], in0=negz[:, b * TILES : (b + 1) * TILES], in1=lse[b][:], op=ALU.add)
+        def dust_min(b, free_bank):
+            nc.vector.tensor_reduce(out=zgap_min[b][:], in_=zgap[b][:], axis=AX.X, op=ALU.min)
+            zturn[b] = bank(free_bank, "zturn_min%d" % b, [P, P])
+            nc.tensor.transpose(zturn[b][:], spread(zgap_min[b][:]), ident[:])
 
         def dust_exp(b):
+            nc.vector.tensor_reduce(out=zleast[b][:], in_=zturn[b][:], axis=AX.X, op=ALU.min)
             nc.scalar.activation(
-                out=ez_col[b][:], in_=zlog[b][:], func=ACT.Exp, scale=-1.0, bias=zleast[b][:], accum_out=zpart[b][:]
+                out=zexp[b][:], in_=zgap[b][:], func=ACT.Exp, scale=-1.0, bias=zleast[b][:], accum_out=zpart[b][:]
             )
 
-        def dust_turn(b, n):
-            zturn[b] = bank(n, "zturn_sum%d" % b, [P, P])
+        def dust_turn(b):
+            zturn[b] = bank(own_bank(b, 0), "zturn_sum%d" % b, [P, P])
             nc.tensor.transpose(zturn[b][:], spread(zpart[b][:]), ident[:])
 
         def dust_sum(b):
@@ -377,52 +355,60 @@ def tile_saladsinkhorndustbinaggregation_kernel(tc, h_bytes, h_scale, wp, z, g, 
         def dust_invert(b):
             nc.vector.reciprocal(out=zinv[b][:], in_=zsum[b][:])
 
-        def dust_scale(b):
+        def dust_scale(b, shares):
             nc.vector.tensor_scalar(
-                out=dust[b][:], in0=ez_col[b][:], scalar1=zinv[b][:], scalar2=float(S - C) / (P if b == 1 else 1.0), op0=ALU.mult, op1=ALU.mult
+                out=dust[b][:], in0=zexp[b][:], scalar1=zinv[b][:], scalar2=float(S - C) / shares, op0=ALU.mult, op1=ALU.mult
             )
 
-        row2 = per_batch("row2", [P, TILES])
+        folded, inv_rows = {}, {}
+        row2 = sbt("row2", [P, TILES], F32)
         total2 = per_batch("total2", [P, TILES])
         row_inv = per_batch("row_inv", [P, TILES])
+        spent_fold = sbt("spent_fold", [P, TILES, P], BF16)
 
-        def row2_sum(b, q):
-            nc.vector.tensor_reduce(out=row2[b][:, q * PACK : (q + 1) * PACK], in_=folded[b, q][:], axis=AX.X, op=ALU.add)
+        def tile_cols(q):
+            return slice(q * PACK, (q + 1) * PACK)
 
-        def row2_total(b, q):
-            cols = slice(q * PACK, (q + 1) * PACK)
-            nc.vector.tensor_tensor(out=total2[b][:, cols], in0=row2[b][:, cols], in1=dust[b][:, cols], op=ALU.add)
+        def fold(b, ch, q):
+            if ch == 0:
+                folded[b, q] = bank(own_bank(b, q), "folded%d%d" % (b, q), [P, PACK, P])
+            for pos in range(PACK):
+                i = q * PACK + pos
+                first, last = ch == 0 and pos == 0, ch == CHUNKS - 1 and pos == PACK - 1
+                add_turned(folded[b, q][:, pos, :], plan[b][:, ch, i * P : (i + 1) * P], first, last)
 
-        def row2_scalar(b, q):
+        def row2_reduce(b, q):
+            nc.vector.tensor_reduce(out=row2[:, tile_cols(q)], in_=folded[b, q][:], axis=AX.X, op=ALU.add)
+
+        def row2_add_dust(b, q):
+            cols = tile_cols(q)
+            nc.vector.tensor_tensor(out=total2[b][:, cols], in0=row2[:, cols], in1=dust[b][:, cols], op=ALU.add)
+
+        def row2_on_scalar(b, q):
             for pos in range(PACK):
                 i = q * PACK + pos
                 nc.scalar.activation(
-                    out=junk_r[b][:, i, :],
+                    out=spent_fold[:, i, :],
                     in_=folded[b, q][:, pos, :],
                     func=ACT.Identity,
                     bias=dust[b][:, i : i + 1],
                     accum_out=total2[b][:, i : i + 1],
                 )
 
-        inv_rows = {}
-
-        def spread_tokens(n, name, src, q):
-            rows = bank(n, name, [P, SPAN])
+        def row2_invert(b, q):
+            nc.vector.reciprocal(out=row_inv[b][:, tile_cols(q)], in_=total2[b][:, tile_cols(q)])
+            inv_rows[b, q] = bank(own_bank(b, PASSES + q), "inv_rows%d%d" % (b, q), [P, SPAN])
             for pos in range(PACK):
                 i = q * PACK + pos
-                nc.tensor.transpose(rows[:, pos * P : (pos + 1) * P], spread(src[:, i : i + 1]), ident[:])
-            return rows
+                nc.tensor.transpose(inv_rows[b, q][:, pos * P : (pos + 1) * P], spread(row_inv[b][:, i : i + 1]), ident[:])
 
-        def row2_invert(b, q):
-            cols = slice(q * PACK, (q + 1) * PACK)
-            nc.vector.reciprocal(out=row_inv[b][:, cols], in_=total2[b][:, cols])
-            inv_rows[b, q] = spread_tokens(late_bank(b, 2 + q), "inv_rows%d%d" % (b, q), row_inv[b], q)
+        pg, pturn, pgrp, agg = {}, {}, {}, {}
 
         def col2_sum(b, ch, q):
-            cols = slice(q * SPAN, (q + 1) * SPAN)
+            part = plan[b][:, ch, pass_cols(q)]
             nc.vector.scalar_tensor_tensor(
-                out=kern[b][:, ch, cols],
-                in0=kern[b][:, ch, cols],
+                out=part,
+                in0=part,
                 scalar=1.0,
                 in1=inv_rows[b, q][:],
                 op0=ALU.mult,
@@ -430,288 +416,183 @@ def tile_saladsinkhorndustbinaggregation_kernel(tc, h_bytes, h_scale, wp, z, g, 
                 accum_out=col_part[1][b][:, ch, q : q + 1],
             )
 
-        pg, pturn, pgrp, p_mx = {}, {}, {}, {}
-
         def assign(b, ch, q):
             pg[b, ch, q] = sbt("pg%d%d%d" % (b, ch, q), [P, SPAN], BF16)
             nc.vector.scalar_tensor_tensor(
                 out=pg[b, ch, q][:].rearrange("p (j r) -> p j r", j=2),
-                in0=kern[b][:, ch, q * SPAN : (q + 1) * SPAN].rearrange("p (j r) -> p j r", j=2),
+                in0=plan[b][:, ch, pass_cols(q)].rearrange("p (j r) -> p j r", j=2),
                 scalar=col_inv[1][b][:, ch : ch + 1],
-                in1=gate_rows[b][:, q * SPAN : (q + 1) * SPAN].rearrange("p (r j) -> p j r", j=2),
+                in1=gate_rows[b][:, pass_cols(q)].rearrange("p (r j) -> p j r", j=2),
                 op0=ALU.mult,
                 op1=ALU.mult,
             )
 
         def p_turn(b, ch, q):
-            pturn[b, ch, q] = bank(late_bank(b, q), "pturn%d%d%d" % (b, ch, q), [P, 2, P])
+            pturn[b, ch, q] = bank(own_bank(b, q), "pturn%d%d%d" % (b, ch, q), [P, 2, P])
             words = pg[b, ch, q][:].bitcast(F32)
-            for u in range(2):
-                nc.tensor.transpose(pturn[b, ch, q][:, u, :], words[:, u * P : (u + 1) * P], ident[:])
+            for j in range(2):
+                nc.tensor.transpose(pturn[b, ch, q][:, j, :], words[:, j * P : (j + 1) * P], ident[:])
 
         def p_group(b, ch, q):
             pgrp[b, ch, q] = sbt("pgrp%d%d%d" % (b, ch, q), [P, SPAN], BF16)
             nc.scalar.copy(
-                out=pgrp[b, ch, q][:].bitcast(F32).rearrange("p (r u) -> p r u", u=2), in_=pturn[b, ch, q][:].rearrange("p u r -> p r u")
+                out=pgrp[b, ch, q][:].bitcast(F32).rearrange("p (c j) -> p c j", j=2),
+                in_=pturn[b, ch, q][:].rearrange("p j c -> p c j"),
             )
-
-        agg = {}
-
-        def p_quant(b, ch, q):
-            codes = sbt("p_codes%d%d%d" % (b, ch, q), [P, P], U32)
-            scales = sbt("p_scales%d%d%d" % (b, ch, q), [P, P], U8)
-            nc.vector.quantize_mx(out=codes[:].bitcast(FP8X4), scales=scales[:], in_=pgrp[b, ch, q][:])
-            p_mx[b, ch, q] = (codes, scales)
-
-        def aggregate(b, ch, q):
-            codes, scales = p_mx[b, ch, q]
-            if q == 0:
-                agg[b, ch] = bank(late_bank(b, 2 + ch), "agg%d%d" % (b, ch), [P, E])
-            nc.tensor.matmul_mx(
-                out=agg[b, ch][:],
-                lhsT=codes[:].bitcast(FP8X4),
-                lhsT_scale=scales[:],
-                rhs=f_codes[b, q][:].bitcast(FP8X4),
-                rhs_scale=f_scales[b, q][:],
-                start=(q == 0),
-                stop=(q == PASSES - 1),
-            )
-
-        sq, root, inv = {}, {}, {}
-
-        def preload_root_table():
-            warm = sbt("warm", [P, 1], F32)
-            nc.scalar.activation(out=warm[:], in_=col_inv[0][B - 1][:, 0:1], func=ACT.Abs_reciprocal_sqrt)
-
-        def norm_square(b, ch):
-            sq[b, ch] = sbt("sq%d%d" % (b, ch), [P, 1], F32)
-            nc.scalar.activation(out=junk_q[b][:, ch, :], in_=agg[b, ch][:], func=ACT.Square, accum_out=sq[b, ch][:])
-
-        def norm_root(b, ch):
-            root[b, ch] = sbt("root%d%d" % (b, ch), [P, 1], F32)
-            nc.scalar.activation(out=root[b, ch][:], in_=sq[b, ch][:], func=ACT.Abs_reciprocal_sqrt, scale=1.0 / E, bias=1e-6)
-
-        def norm_inverse(b, ch):
-            inv[b, ch] = sbt("inv%d%d" % (b, ch), [P, 1], F32)
-            nc.vector.reciprocal(out=root[b, ch][:], in_=root[b, ch][:])
-
-        def store(b, ch, parts, on_scalar=False):
-            for part in range(parts):
-                cols = slice(part * E // parts, (part + 1) * E // parts)
-                y = sbt("y%d%d%d" % (b, ch, part), [P, E // parts], F32)
-                if on_scalar:
-                    nc.scalar.activation(out=y[:], in_=agg[b, ch][:, cols], func=ACT.Copy, scale=root[b, ch][:])
-                else:
-                    nc.vector.tensor_scalar(out=y[:], in0=agg[b, ch][:, cols], scalar1=root[b, ch][:], scalar2=None, op0=ALU.mult)
-                nc.sync.dma_start(out=out[b, ch * P : (ch + 1) * P, cols], in_=y[:])
-
-        def weave(first, second):
-            for n in range(max(len(first), len(second))):
-                for steps in (first, second):
-                    if n < len(steps):
-                        steps[n]()
-
-        def step(fn, *args):
-            return lambda: fn(*args)
-
-        def chain(*steps):
-            return lambda: [s() for s in steps]
-
-
-        def copy_pair(b, k):
-            row_copy(b, 2 * k)
-            row_copy(b, 2 * k + 1)
-
-        def sum_pair(b, k):
-            row_sum(b, 2 * k)
-            row_sum(b, 2 * k + 1)
-
-        def widen_pair(b, k):
-            h_widen(b, 2 * k)
-            h_widen(b, 2 * k + 1)
-            h_turn(b, k)
-            h_group(b, k)
-
-        def quant_pair(b, k):
-            h_quant(b, k)
-            score_matmul(b, k)
-
-        def turn_half(b, q):
-            for i in range(q * PACK, (q + 1) * PACK):
-                turn_scores(b, i)
-
-        def add_chunk(b, ch):
-            for q in range(PASSES):
-                add_lse(b, ch, q)
-
-        def exp_chunk(b, ch):
-            col_least_join(b, ch)
-            for q in range(PASSES):
-                kernel_exp(b, ch, q)
-
-        def scale_chunk(b, ch):
-            for q in range(PASSES):
-                col_scale(b, ch, q)
-
-        def rows2(b, q):
-            if b == 1:
-                row2_scalar(b, q)
-            else:
-                row2_sum(b, q)
-
-        def total_rows2(b, q):
-            if b == 0:
-                row2_total(b, q)
-
-        def invert_rows2(b, q):
-            row2_invert(b, q)
 
         def p_move(b, ch, q):
             p_turn(b, ch, q)
             p_group(b, ch, q)
 
-        def p_pass(b, ch, q):
-            p_quant(b, ch, q)
-            aggregate(b, ch, q)
+        def aggregate(b, ch, q):
+            p_mx = quantize("p%d%d%d" % (b, ch, q), pgrp[b, ch, q][:], P)
+            if q == 0:
+                agg[b, ch] = bank(own_bank(b, PASSES + ch), "agg%d%d" % (b, ch), [P, E])
+            matmul_mx(agg[b, ch][:], p_mx, slice(0, P), mx["f", b, q], q == 0, q == PASSES - 1)
 
-        f_todo = [(b, q, part) for b in reversed(range(B)) for q in reversed(range(PASSES)) for part in reversed(range(4))]
+        squares, norm = {}, {}
+        spent_square = per_batch("spent_square", [P, CHUNKS, E], BF16)
 
-        def f_parts(n):
-            for k in range(n):
-                f_group(*f_todo[-1])
-                f_todo.remove(f_todo[-1])
+        def norm_square(b, ch):
+            squares[b, ch] = sbt("squares%d%d" % (b, ch), [P, 1], F32)
+            nc.scalar.activation(out=spent_square[b][:, ch, :], in_=agg[b, ch][:], func=ACT.Square, accum_out=squares[b, ch][:])
 
+        def norm_root(b, ch):
+            norm[b, ch] = sbt("norm%d%d" % (b, ch), [P, 1], F32)
+            nc.scalar.activation(
+                out=norm[b, ch][:], in_=squares[b, ch][:], func=ACT.Abs_reciprocal_sqrt, scale=1.0 / E, bias=1e-6
+            )
+
+        def store(b, ch, parts=1, on_scalar=False):
+            for part in range(parts):
+                cols = slice(part * E // parts, (part + 1) * E // parts)
+                y = sbt("y%d%d%d" % (b, ch, part), [P, E // parts], F32)
+                if on_scalar:
+                    nc.scalar.activation(out=y[:], in_=agg[b, ch][:, cols], func=ACT.Copy, scale=norm[b, ch][:])
+                else:
+                    nc.vector.tensor_scalar(out=y[:], in0=agg[b, ch][:, cols], scalar1=norm[b, ch][:], scalar2=None, op0=ALU.mult)
+                nc.sync.dma_start(out=out[b, ch * P : (ch + 1) * P, cols], in_=y[:])
+
+        scalar_copy, vector_copy = nc.scalar.copy, nc.vector.tensor_copy
+
+
+        lag = 2
+        steps = B * PAIRS
         w_group()
-        widen_pair(0, 0)
-        f_parts(1)
-        w_quant()
-        widen_pair(0, 1)
-        f_parts(2)
-        h_widen(0, 4)
-        quant_pair(0, 0)
-        h_widen(0, 5)
-        h_turn(0, 2)
-        h_group(0, 2)
-        quant_pair(0, 1)
-        copy_pair(0, 0)
-        sum_pair(0, 0)
-        f_parts(1)
-        widen_pair(0, 3)
-        quant_pair(0, 2)
-        copy_pair(0, 1)
-        sum_pair(0, 1)
-        f_parts(1)
-        h_widen(1, 0)
-        quant_pair(0, 3)
-        turn_half(0, 0)
-        copy_pair(0, 2)
-        sum_pair(0, 2)
-        h_widen(1, 1)
-        h_turn(1, 0)
-        copy_pair(0, 3)
-        sum_pair(0, 3)
-        h_group(1, 0)
-        turn_half(0, 1)
-        h_widen(1, 2)
-        dust_gap(0)
-        h_widen(1, 3)
-        h_turn(1, 1)
-        log0 = log_steps(0)
-        log0[0]()
-        f_parts(1)
-        h_group(1, 1)
-        quant_pair(1, 0)
-        log0[1]()
-        h_widen(1, 4)
-        f_parts(1)
-        weave(log0[2:], [
-            chain(step(h_widen, 1, 5), step(h_turn, 1, 2), step(h_group, 1, 2), step(f_parts, 2)),
-            step(quant_pair, 1, 1),
-            chain(step(h_widen, 1, 6)),
-            chain(step(h_widen, 1, 7), step(h_turn, 1, 3)),
-            chain(step(row_copy, 1, 0)),
-            chain(step(row_copy, 1, 1), step(h_group, 1, 3), step(sum_pair, 1, 0)),
-            step(quant_pair, 1, 2),
-            ])
-        copy_pair(1, 1)
-        sum_pair(1, 1)
-        f_parts(1)
-        quant_pair(1, 3)
-        add_chunk(0, 0)
-        copy_pair(1, 2)
-        dust_log(0)
-        sum_pair(1, 2)
-        copy_pair(1, 3)
-        sum_pair(1, 3)
-        add_chunk(0, 1)
-        dust_min(0, 6)
-        col_least(0, 0, 0)
-        dust_gap(1)
-        log1 = log_steps(1)
-        log1[0]()
-        f_parts(1)
-        log1[1]()
-        col_least(0, 0, 1)
-        log1[2]()
-        turn_half(1, 0)
-        turn_half(1, 1)
-        exp_chunk(0, 0)
-        log1[3]()
-        dust_least(0)
-        dust_exp(0)
-        log1[4]()
-        col_least(0, 1, 0)
-        log1[5]()
-        col_least(0, 1, 1)
-        log1[6]()
-        col_join(0, 0, 0)
-        exp_chunk(0, 1)
-        log1[7]()
-        col_invert(0, 0, 0)
-        scale_chunk(0, 0)
-        dust_turn(0, 0)
-        log1[8]()
-        dust_sum(0)
-        log1[9]()
-        add_chunk(1, 0)
+        for n in range(steps):
+            (nb, nk), (ob, ok) = divmod(n, PAIRS), divmod(n - lag, PAIRS)
+            if n >= lag:
+                score_pair(ob, ok)
+            ride()
+            if n == PAIRS + lag:
+                riders.extend(log_steps(0) + [lambda: dust_gap(0)])
+            if lag < n <= PAIRS + lag:
+                turn_scores(0, 2 * (n - lag - 1))
+                turn_scores(0, 2 * (n - lag - 1) + 1)
+            for a in range(2):
+                h_widen(nb, 2 * nk + a)
+                ride()
+            if n == lag - 1:
+                w_quant()
+            h_turn(nb, nk)
+            if n >= lag:
+                for a in range(2):
+                    row_copy(ob, 2 * ok + a)
+                    ride()
+            if n == steps - 1:
+                h_group(nb, nk)
+            if n >= lag:
+                row_sums(ob, ok)
+            if n < steps - 1:
+                h_group(nb, nk)
+            if n > 0:
+                f_parts(1 if n >= lag else 2, scalar_copy)
+
+        score_pair(1, 2)
+        ride()
+        add_lse(0, 0, 0)
         f_quant(0, 0)
+        score_pair(1, 3)
+        ride()
+        add_lse(0, 0, 1)
+        for k in (2, 3):
+            row_copy(1, 2 * k)
+            row_copy(1, 2 * k + 1)
+            row_sums(1, k)
+            if k == 2:
+                f_parts(1, scalar_copy)
+                f_parts(2, vector_copy)
+        add_lse(0, 1, 0)
+        add_lse(0, 1, 1)
+        dust_min(0, 6)
+
+        col_least(0, 0, 0)
+        riders.extend(log_steps(1))
+        ride()
+        f_parts(1, scalar_copy)
+        ride()
+        col_least(0, 0, 1)
+        ride()
+        for i in range(TILES):
+            turn_scores(1, i)
+        col_exp(0, 0)
+        ride()
+        dust_exp(0)
+        ride()
+        for q in range(PASSES):
+            col_least(0, 1, q)
+            ride()
+        col_join(0, 0, 0)
+        col_exp(0, 1)
+        ride()
+        col_invert(0, 0, 0)
+        col_scale(0, 0)
+        dust_turn(0)
+        ride()
+        dust_sum(0)
+        ride()
+        add_lse(1, 0, 0)
+        add_lse(1, 0, 1)
+        f_quant(0, 1)
+        f_quant(1, 0)
         col_join(0, 0, 1)
+        dust_gap(1)
         dust_invert(0)
-        dust_log(1)
         col_invert(0, 0, 1)
-        scale_chunk(0, 1)
-        f_parts(1)
-        dust_scale(0)
+        col_scale(0, 1)
+        f_parts(1, scalar_copy)
+        dust_scale(0, 1)
+
         fold(0, 0, 0)
-        add_chunk(1, 1)
+        add_lse(1, 1, 0)
+        add_lse(1, 1, 1)
         fold(0, 1, 0)
         dust_min(1, 3)
         fold(0, 0, 1)
         fold(0, 1, 1)
         col_least(1, 0, 0)
         col_least(1, 0, 1)
-        f_quant(0, 1)
-        exp_chunk(1, 0)
+        f_parts(1, vector_copy)
+        col_exp(1, 0)
         col_least(1, 1, 0)
         col_least(1, 1, 1)
-        rows2(0, 0)
-        exp_chunk(1, 1)
-        dust_least(1)
+        row2_reduce(0, 0)
+        col_exp(1, 1)
         dust_exp(1)
-        total_rows2(0, 0)
-        rows2(0, 1)
-        invert_rows2(0, 0)
+        row2_add_dust(0, 0)
+        row2_reduce(0, 1)
+        row2_invert(0, 0)
         col_join(1, 0, 0)
-        total_rows2(0, 1)
+        row2_add_dust(0, 1)
         col_invert(1, 0, 0)
-        scale_chunk(1, 0)
-        invert_rows2(0, 1)
+        col_scale(1, 0)
+        row2_invert(0, 1)
         col_join(1, 0, 1)
-        dust_turn(1, 4)
-        f_quant(1, 0)
+        dust_turn(1)
         col_invert(1, 0, 1)
-        scale_chunk(1, 1)
-        f_parts(2)
+        col_scale(1, 1)
+        f_parts(1, scalar_copy)
+
         col2_sum(0, 0, 0)
         dust_sum(1)
         fold(1, 0, 0)
@@ -719,13 +600,12 @@ def tile_saladsinkhorndustbinaggregation_kernel(tc, h_bytes, h_scale, wp, z, g, 
         dust_invert(1)
         fold(1, 1, 0)
         col2_sum(0, 1, 0)
-        dust_scale(1)
+        dust_scale(1, P)
         col_join(0, 1, 0)
         fold(1, 0, 1)
         fold(1, 1, 1)
-        rows2(1, 0)
-        rows2(1, 1)
-        f_parts(2)
+        row2_on_scalar(1, 0)
+        row2_on_scalar(1, 1)
         col2_sum(0, 1, 1)
         col_invert(0, 1, 0)
         col_join(0, 1, 1)
@@ -733,52 +613,52 @@ def tile_saladsinkhorndustbinaggregation_kernel(tc, h_bytes, h_scale, wp, z, g, 
         col_invert(0, 1, 1)
         p_turn(0, 0, 0)
         assign(0, 0, 1)
-        invert_rows2(1, 0)
+        row2_invert(1, 0)
         p_turn(0, 0, 1)
         p_group(0, 0, 0)
+        f_parts(1, scalar_copy)
         p_group(0, 0, 1)
         assign(0, 1, 0)
-        invert_rows2(1, 1)
+        row2_invert(1, 1)
         assign(0, 1, 1)
         p_move(0, 1, 0)
         p_move(0, 1, 1)
-        preload_root_table()
+
         col2_sum(1, 0, 0)
-        f_quant(1, 1)
-        p_pass(0, 0, 0)
-        p_pass(0, 0, 1)
+        aggregate(0, 0, 0)
+        aggregate(0, 0, 1)
         col2_sum(1, 0, 1)
-        p_pass(0, 1, 0)
+        aggregate(0, 1, 0)
         col_join(1, 1, 0)
         col2_sum(1, 1, 0)
         col_invert(1, 1, 0)
-        p_pass(0, 1, 1)
+        aggregate(0, 1, 1)
         norm_square(0, 0)
         col2_sum(1, 1, 1)
         norm_root(0, 0)
-        norm_square(0, 1)
         assign(1, 0, 0)
         col_join(1, 1, 1)
         p_move(1, 0, 0)
-        norm_root(0, 1)
         assign(1, 0, 1)
         col_invert(1, 1, 1)
         p_move(1, 0, 1)
-        store(0, 0, 1, True)
+        norm_square(0, 1)
         assign(1, 1, 0)
-        p_quant(1, 0, 0)
-        p_move(1, 1, 0)
         aggregate(1, 0, 0)
+        p_move(1, 1, 0)
+        norm_root(0, 1)
         assign(1, 1, 1)
-        p_quant(1, 0, 1)
         p_move(1, 1, 1)
+
+        store(0, 0, on_scalar=True)
+        f_quant(1, 1)
         aggregate(1, 0, 1)
-        p_pass(1, 1, 0)
-        p_pass(1, 1, 1)
+        aggregate(1, 1, 0)
+        aggregate(1, 1, 1)
         norm_square(1, 0)
-        store(0, 1, 1)
+        store(0, 1)
         norm_root(1, 0)
         norm_square(1, 1)
-        store(1, 0, 1)
+        store(1, 0)
         norm_root(1, 1)
-        store(1, 1, 2)
+        store(1, 1, parts=2)

import math
from contextlib import ExitStack

import concourse.mybir as mybir
from concourse.masks import make_identity

B, S, H, C, E = 2, 1024, 512, 256, 512
FLOPS = 2 * B * S * H * C + 2 * B * S * C * E

F32 = mybir.dt.float32
BF16 = mybir.dt.bfloat16
I32 = mybir.dt.int32
U32 = mybir.dt.uint32
U8 = mybir.dt.uint8
FP8 = mybir.dt.float8_e4m3fn
FP8X4 = mybir.dt.float8_e4m3fn_x4
ALU = mybir.AluOpType
ACT = mybir.ActivationFunctionType
AX = mybir.AxisListType

P = 128
PACK = 4
SPAN = P * PACK
PASSES = S // SPAN
TILES = PASSES * PACK
PAIRS = TILES // 2
CHUNKS = C // P
ROW = C + 8
F_PARTS = 4
LN2 = math.log(2.0)
LOG2_MIDDLE = 0.043


def tile_saladsinkhorndustbinaggregation_kernel(tc, h_bytes, h_scale, wp, z, g, f, out):
    nc = tc.nc
    with ExitStack() as ctx:
        sb = ctx.enter_context(tc.tile_pool(name="sb", bufs=1))
        ps = ctx.enter_context(tc.psum_pool(name="ps", bufs=1))
        ctx.enter_context(tc.manual_schedule())

        def sbt(name, shape, dtype):
            return sb.tile(shape, dtype, name=name, tag=name, align_bytes=64)

        def per_batch(name, shape, dtype=F32):
            return [sbt("%s%d" % (name, b), shape, dtype) for b in range(B)]

        def bank(n, name, shape):
            return ps.tile(shape, F32, name=name, tag="bank%d" % n)

        def own_bank(b, n):
            return 4 * b + n

        def spread(col):
            return col.to_broadcast([P, P])

        hbytes, fraw = {}, {}

        def load_h(b, q):
            hbytes[b, q] = sbt("hbytes%d%d" % (b, q), [P, 2, 2 * H], U8)
            nc.sync.dma_start(
                out=hbytes[b, q][:],
                in_=h_bytes[b, q * SPAN : (q + 1) * SPAN, :].rearrange("(a p j) k -> p a (j k)", a=2, j=2),
            )

        def load_f(b, q):
            fraw[b, q] = sbt("fraw%d%d" % (b, q), [P, PACK, E], BF16)
            nc.sync.dma_start(
                out=fraw[b, q][:], in_=f[b, q * SPAN : (q + 1) * SPAN, :].rearrange("(p j) e -> p j e", j=PACK)
            )

        hs = sbt("hs", [P, PACK], F32)
        nc.sync.dma_start(out=hs[:], in_=h_scale.rearrange("a o (p t) -> p (a o t)", t=PACK))
        wraw = sbt("wraw", [P, PACK, C], BF16)
        nc.sync.dma_start(out=wraw[:], in_=wp.rearrange("(p j) c -> p j c", j=PACK))
        load_h(0, 0)
        zrows = sbt("zrows", [P, P], F32)
        nc.vector.memset(zrows[:], 0.0)
        nc.sync.dma_start(out=zrows[0 : B * PAIRS, :].bitcast(BF16), in_=z.rearrange("b (a n) -> (b a) n", n=2 * P))
        load_h(0, 1)
        load_f(0, 0)
        load_f(0, 1)
        load_h(1, 0)
        load_h(1, 1)
        load_f(1, 0)
        load_f(1, 1)
        gate_rows = per_batch("gate_rows", [P, S], BF16)
        for b in range(B):
            nc.sync.dma_start(out=gate_rows[b][:], in_=g[b].partition_broadcast(P))

        ident = sbt("ident", [P, P], F32)
        make_identity(nc, ident[:])

        sc_ps = bank(7, "sc_ps", [P, PACK, P])
        for t in range(PACK):
            nc.tensor.transpose(sc_ps[:, t, :], spread(hs[:, t : t + 1]), ident[:])
        scale_rows = sbt("scale_rows", [P, H], F32)
        nc.scalar.activation(
            out=scale_rows[:].rearrange("m (p t) -> m p t", t=PACK),
            in_=sc_ps[:].rearrange("m t p -> m p t"),
            func=ACT.Copy,
        )

        z_ps = bank(0, "z_ps", [P, P])
        nc.tensor.transpose(z_ps[:], zrows[:], ident[:])
        negz = sbt("negz", [P, B * TILES], F32)
        nc.scalar.activation(
            out=negz[:].rearrange("p (q j a) -> p q j a", j=2, a=2),
            in_=z_ps[:, 0 : B * PAIRS].bitcast(BF16).rearrange("p (q a j) -> p q j a", j=2, a=2),
            func=ACT.Copy,
            scale=-1.0,
        )
        negt = per_batch("negt", [P, TILES, ROW])
        for b in range(B):
            nc.gpsimd.tensor_copy(out=negt[b][:, :, C], in_=negz[:, b * TILES : (b + 1) * TILES])

        def quantize(name, src, words):
            codes = sbt(name + "_codes", [P, words], U32)
            scales = sbt(name + "_scales", [P, words], U8)
            nc.vector.quantize_mx(out=codes[:].bitcast(FP8X4), scales=scales[:], in_=src)
            return codes, scales

        def matmul_mx(dst, lhs, lhs_cols, rhs, start, stop):
            nc.tensor.matmul_mx(
                out=dst,
                lhsT=lhs[0][:, lhs_cols].bitcast(FP8X4),
                lhsT_scale=lhs[1][:, lhs_cols],
                rhs=rhs[0][:].bitcast(FP8X4),
                rhs_scale=rhs[1][:],
                start=start,
                stop=stop,
            )

        def add_turned(dst, src, start, stop):
            nc.tensor.matmul(dst, lhsT=src, rhs=ident[:], start=start, stop=stop, is_transpose=True)

        mx = {}
        hwide, hturn, hgrp, scores = {}, {}, {}, {}
        wgrp = sbt("wgrp", [P, C, PACK], BF16)

        def w_group():
            nc.vector.tensor_copy(out=wgrp[:], in_=wraw[:].rearrange("p j c -> p c j"))

        def w_quant():
            mx["w"] = quantize("w", wgrp[:].rearrange("p c j -> p (c j)"), C)

        def h_widen(b, i):
            q, j, a = i // PACK, (i // 2) % 2, i % 2
            hwide[b, i] = sbt("hwide%d%d" % (b, i), [P, H], BF16)
            nc.vector.tensor_tensor(
                out=hwide[b, i][:], in0=hbytes[b, q][:, a, j * H : (j + 1) * H].bitcast(FP8), in1=scale_rows[:], op=ALU.mult
            )

        def h_turn(b, k):
            hturn[b, k] = bank(4 + k % 2, "hturn%d%d" % (b, k), [P, 2, 2, P])
            for a in range(2):
                words = hwide[b, 2 * k + a][:].bitcast(F32)
                for u in range(2):
                    nc.tensor.transpose(hturn[b, k][:, a, u, :], words[:, u : H // 2 : 2], ident[:])

        def h_group(b, k):
            hgrp[b, k] = sbt("hgrp%d%d" % (b, k), [P, 2 * SPAN], BF16)
            nc.scalar.copy(
                out=hgrp[b, k][:].bitcast(F32).rearrange("p (a r u) -> p a r u", a=2, u=2),
                in_=hturn[b, k][:].rearrange("p a u r -> p a r u"),
            )

        def score_pair(b, k):
            h_mx = quantize("h%d%d" % (b, k), hgrp[b, k][:], 2 * P)
            scores[b, k] = bank(6 + k % 2, "scores%d%d" % (b, k), [P, 2, C])
            for a in range(2):
                matmul_mx(scores[b, k][:, a, :], h_mx, slice(a * P, (a + 1) * P), mx["w"], True, True)

        fgrp = {}
        f_todo = [(b, q, part) for b in range(B) for q in range(PASSES) for part in range(F_PARTS)]

        def f_parts(count, copy):
            for b, q, part in f_todo[0:count]:
                if part == 0:
                    fgrp[b, q] = sbt("fgrp%d%d" % (b, q), [P, E, 2, 2], BF16)
                cols = slice(part * E // F_PARTS, (part + 1) * E // F_PARTS)
                copy(
                    out=fgrp[b, q][:, cols, :, :].rearrange("p (c i) u e -> p c u e i", i=PACK),
                    in_=fraw[b, q][:, :, cols].rearrange("p (e u) (c i) -> p c u e i", u=2, i=PACK),
                )
                f_todo.remove((b, q, part))

        def f_quant(b, q):
            mx["f", b, q] = quantize("f%d%d" % (b, q), fgrp[b, q][:].rearrange("p n u e -> p (n u e)"), E)

        negm = per_batch("negm", [P, TILES])
        total = per_batch("total", [P, TILES])
        spent_exp = per_batch("spent_exp", [P, TILES, ROW], BF16)

        def row_copy(b, i):
            nc.vector.tensor_scalar(
                out=negt[b][:, i, 0:C],
                in0=scores[b, i // 2][:, i % 2, :],
                scalar1=-1.0,
                scalar2=negz[:, b * TILES + i : b * TILES + i + 1],
                op0=ALU.mult,
                op1=ALU.min,
                accum_out=negm[b][:, i : i + 1],
            )

        def row_sums(b, k):
            for i in (2 * k, 2 * k + 1):
                nc.scalar.activation(
                    out=spent_exp[b][:, i, 0 : C + 1],
                    in_=negt[b][:, i, 0 : C + 1],
                    func=ACT.Exp,
                    scale=-1.0,
                    bias=negm[b][:, i : i + 1],
                    accum_out=total[b][:, i : i + 1],
                )

        guess = per_batch("guess", [P, TILES])
        back = per_batch("back", [P, TILES])
        base = per_batch("base", [P, TILES])
        ratio = per_batch("ratio", [P, TILES])
        rest = per_batch("rest", [P, TILES])
        series = per_batch("series", [P, TILES])
        lse = per_batch("lse", [P, TILES])

        def log_steps(b):
            def first_guess():
                nc.vector.tensor_scalar(
                    out=guess[b][:],
                    in0=total[b][:].bitcast(I32),
                    scalar1=LN2 / 2.0**23,
                    scalar2=-(127.0 - LOG2_MIDDLE) * LN2,
                    op0=ALU.mult,
                    op1=ALU.add,
                )
                nc.scalar.activation(out=back[b][:], in_=guess[b][:], func=ACT.Exp, scale=-1.0)

            def horner(src, c):
                return lambda: nc.vector.scalar_tensor_tensor(
                    out=series[b][:], in0=src[:], scalar=c, in1=rest[b][:], op0=ALU.add, op1=ALU.mult
                )

            return [
                first_guess,
                lambda: nc.vector.tensor_tensor(out=base[b][:], in0=guess[b][:], in1=negm[b][:], op=ALU.subtract),
                lambda: nc.vector.tensor_tensor(out=ratio[b][:], in0=total[b][:], in1=back[b][:], op=ALU.mult),
                lambda: nc.vector.tensor_scalar(out=rest[b][:], in0=ratio[b][:], scalar1=-1.0, scalar2=None, op0=ALU.add),
                horner(rest[b], -6.0 / 5.0),
                horner(series[b], 6.0 / 4.0),
                horner(series[b], -6.0 / 3.0),
                horner(series[b], 6.0 / 2.0),
                horner(series[b], -6.0),
                lambda: nc.vector.scalar_tensor_tensor(
                    out=lse[b][:], in0=series[b][:], scalar=-1.0 / 6.0, in1=base[b][:], op0=ALU.mult, op1=ALU.add
                ),
            ]

        riders = []

        def ride():
            for rider in riders[0:1]:
                rider()
                riders.remove(rider)

        gaps = {}

        def turn_scores(b, i):
            q, pos = divmod(i, PACK)
            for ch in range(CHUNKS):
                if pos == 0:
                    gaps[b, ch, q] = bank(own_bank(b, CHUNKS * q + ch), "gaps%d%d%d" % (b, ch, q), [P, PACK, P])
                add_turned(gaps[b, ch, q][:, pos, :], negt[b][:, i, ch * P : (ch + 1) * P], pos == 0, False)

        def add_lse(b, ch, q):
            for pos in range(PACK):
                i = q * PACK + pos
                add_turned(gaps[b, ch, q][:, pos, :], spread(lse[b][:, i : i + 1]), False, pos == PACK - 1)

        least_part = per_batch("least_part", [P, CHUNKS, PASSES])
        least = per_batch("least", [P, CHUNKS])
        plan = per_batch("plan", [P, CHUNKS, S])
        col_part = [per_batch("col_part%d" % r, [P, CHUNKS, PASSES]) for r in range(2)]
        col_sum = [per_batch("col_sum%d" % r, [P, CHUNKS]) for r in range(2)]
        col_inv = [per_batch("col_inv%d" % r, [P, CHUNKS]) for r in range(2)]

        def pass_cols(q):
            return slice(q * SPAN, (q + 1) * SPAN)

        def col_least(b, ch, q):
            nc.vector.tensor_reduce(
                out=least_part[b][:, ch, q : q + 1], in_=gaps[b, ch, q][:].rearrange("p a r -> p (a r)"), axis=AX.X, op=ALU.min
            )

        def col_exp(b, ch):
            nc.vector.tensor_tensor(
                out=least[b][:, ch : ch + 1], in0=least_part[b][:, ch, 0:1], in1=least_part[b][:, ch, 1:2], op=ALU.min
            )
            for q in range(PASSES):
                nc.scalar.activation(
                    out=plan[b][:, ch, pass_cols(q)],
                    in_=gaps[b, ch, q][:].rearrange("p a r -> p (a r)"),
                    func=ACT.Exp,
                    scale=-1.0,
                    bias=least[b][:, ch : ch + 1],
                    accum_out=col_part[0][b][:, ch, q : q + 1],
                )

        def col_join(b, r, ch):
            nc.vector.tensor_scalar(
                out=col_sum[r][b][:, ch : ch + 1],
                in0=col_part[r][b][:, ch, 0:1],
                scalar1=col_part[r][b][:, ch, 1:2],
                scalar2=1.0 if r == 0 else 1.0 / math.sqrt(S),
                op0=ALU.add,
                op1=ALU.mult,
            )

        def col_invert(b, r, ch):
            nc.vector.reciprocal(out=col_inv[r][b][:, ch : ch + 1], in_=col_sum[r][b][:, ch : ch + 1])

        def col_scale(b, ch):
            for q in range(PASSES):
                part = plan[b][:, ch, pass_cols(q)]
                nc.scalar.activation(out=part, in_=part, func=ACT.Copy, scale=col_inv[0][b][:, ch : ch + 1])

        zgap = per_batch("zgap", [P, TILES])
        zgap_min = per_batch("zgap_min", [P, 1])
        zleast = per_batch("zleast", [P, 1])
        zexp = per_batch("zexp", [P, TILES])
        zpart = per_batch("zpart", [P, 1])
        zsum = per_batch("zsum", [P, 1])
        zinv = per_batch("zinv", [P, 1])
        dust = per_batch("dust", [P, TILES])
        zturn = {}

        def dust_gap(b):
            nc.vector.tensor_tensor(out=zgap[b][:], in0=negz[:, b * TILES : (b + 1) * TILES], in1=lse[b][:], op=ALU.add)

        def dust_min(b, free_bank):
            nc.vector.tensor_reduce(out=zgap_min[b][:], in_=zgap[b][:], axis=AX.X, op=ALU.min)
            zturn[b] = bank(free_bank, "zturn_min%d" % b, [P, P])
            nc.tensor.transpose(zturn[b][:], spread(zgap_min[b][:]), ident[:])

        def dust_exp(b):
            nc.vector.tensor_reduce(out=zleast[b][:], in_=zturn[b][:], axis=AX.X, op=ALU.min)
            nc.scalar.activation(
                out=zexp[b][:], in_=zgap[b][:], func=ACT.Exp, scale=-1.0, bias=zleast[b][:], accum_out=zpart[b][:]
            )

        def dust_turn(b):
            zturn[b] = bank(own_bank(b, 0), "zturn_sum%d" % b, [P, P])
            nc.tensor.transpose(zturn[b][:], spread(zpart[b][:]), ident[:])

        def dust_sum(b):
            nc.vector.tensor_reduce(out=zsum[b][:], in_=zturn[b][:], axis=AX.X, op=ALU.add)

        def dust_invert(b):
            nc.vector.reciprocal(out=zinv[b][:], in_=zsum[b][:])

        def dust_scale(b, shares):
            nc.vector.tensor_scalar(
                out=dust[b][:], in0=zexp[b][:], scalar1=zinv[b][:], scalar2=float(S - C) / shares, op0=ALU.mult, op1=ALU.mult
            )

        folded, inv_rows = {}, {}
        row2 = sbt("row2", [P, TILES], F32)
        total2 = per_batch("total2", [P, TILES])
        row_inv = per_batch("row_inv", [P, TILES])
        spent_fold = sbt("spent_fold", [P, TILES, P], BF16)

        def tile_cols(q):
            return slice(q * PACK, (q + 1) * PACK)

        def fold(b, ch, q):
            if ch == 0:
                folded[b, q] = bank(own_bank(b, q), "folded%d%d" % (b, q), [P, PACK, P])
            for pos in range(PACK):
                i = q * PACK + pos
                first, last = ch == 0 and pos == 0, ch == CHUNKS - 1 and pos == PACK - 1
                add_turned(folded[b, q][:, pos, :], plan[b][:, ch, i * P : (i + 1) * P], first, last)

        def row2_reduce(b, q):
            nc.vector.tensor_reduce(out=row2[:, tile_cols(q)], in_=folded[b, q][:], axis=AX.X, op=ALU.add)

        def row2_add_dust(b, q):
            cols = tile_cols(q)
            nc.vector.tensor_tensor(out=total2[b][:, cols], in0=row2[:, cols], in1=dust[b][:, cols], op=ALU.add)

        def row2_on_scalar(b, q):
            for pos in range(PACK):
                i = q * PACK + pos
                nc.scalar.activation(
                    out=spent_fold[:, i, :],
                    in_=folded[b, q][:, pos, :],
                    func=ACT.Identity,
                    bias=dust[b][:, i : i + 1],
                    accum_out=total2[b][:, i : i + 1],
                )

        def row2_invert(b, q):
            nc.vector.reciprocal(out=row_inv[b][:, tile_cols(q)], in_=total2[b][:, tile_cols(q)])
            inv_rows[b, q] = bank(own_bank(b, PASSES + q), "inv_rows%d%d" % (b, q), [P, SPAN])
            for pos in range(PACK):
                i = q * PACK + pos
                nc.tensor.transpose(inv_rows[b, q][:, pos * P : (pos + 1) * P], spread(row_inv[b][:, i : i + 1]), ident[:])

        pg, pturn, pgrp, agg = {}, {}, {}, {}

        def col2_sum(b, ch, q):
            part = plan[b][:, ch, pass_cols(q)]
            nc.vector.scalar_tensor_tensor(
                out=part,
                in0=part,
                scalar=1.0,
                in1=inv_rows[b, q][:],
                op0=ALU.mult,
                op1=ALU.mult,
                accum_out=col_part[1][b][:, ch, q : q + 1],
            )

        def assign(b, ch, q):
            pg[b, ch, q] = sbt("pg%d%d%d" % (b, ch, q), [P, SPAN], BF16)
            nc.vector.scalar_tensor_tensor(
                out=pg[b, ch, q][:].rearrange("p (j r) -> p j r", j=2),
                in0=plan[b][:, ch, pass_cols(q)].rearrange("p (j r) -> p j r", j=2),
                scalar=col_inv[1][b][:, ch : ch + 1],
                in1=gate_rows[b][:, pass_cols(q)].rearrange("p (r j) -> p j r", j=2),
                op0=ALU.mult,
                op1=ALU.mult,
            )

        def p_turn(b, ch, q):
            pturn[b, ch, q] = bank(own_bank(b, q), "pturn%d%d%d" % (b, ch, q), [P, 2, P])
            words = pg[b, ch, q][:].bitcast(F32)
            for j in range(2):
                nc.tensor.transpose(pturn[b, ch, q][:, j, :], words[:, j * P : (j + 1) * P], ident[:])

        def p_group(b, ch, q):
            pgrp[b, ch, q] = sbt("pgrp%d%d%d" % (b, ch, q), [P, SPAN], BF16)
            nc.scalar.copy(
                out=pgrp[b, ch, q][:].bitcast(F32).rearrange("p (c j) -> p c j", j=2),
                in_=pturn[b, ch, q][:].rearrange("p j c -> p c j"),
            )

        def p_move(b, ch, q):
            p_turn(b, ch, q)
            p_group(b, ch, q)

        def aggregate(b, ch, q):
            p_mx = quantize("p%d%d%d" % (b, ch, q), pgrp[b, ch, q][:], P)
            if q == 0:
                agg[b, ch] = bank(own_bank(b, PASSES + ch), "agg%d%d" % (b, ch), [P, E])
            matmul_mx(agg[b, ch][:], p_mx, slice(0, P), mx["f", b, q], q == 0, q == PASSES - 1)

        squares, norm = {}, {}
        spent_square = per_batch("spent_square", [P, CHUNKS, E], BF16)

        def norm_square(b, ch):
            squares[b, ch] = sbt("squares%d%d" % (b, ch), [P, 1], F32)
            nc.scalar.activation(out=spent_square[b][:, ch, :], in_=agg[b, ch][:], func=ACT.Square, accum_out=squares[b, ch][:])

        def norm_root(b, ch):
            norm[b, ch] = sbt("norm%d%d" % (b, ch), [P, 1], F32)
            nc.scalar.activation(
                out=norm[b, ch][:], in_=squares[b, ch][:], func=ACT.Abs_reciprocal_sqrt, scale=1.0 / E, bias=1e-6
            )

        def store(b, ch, parts=1, on_scalar=False):
            for part in range(parts):
                cols = slice(part * E // parts, (part + 1) * E // parts)
                y = sbt("y%d%d%d" % (b, ch, part), [P, E // parts], F32)
                if on_scalar:
                    nc.scalar.activation(out=y[:], in_=agg[b, ch][:, cols], func=ACT.Copy, scale=norm[b, ch][:])
                else:
                    nc.vector.tensor_scalar(out=y[:], in0=agg[b, ch][:, cols], scalar1=norm[b, ch][:], scalar2=None, op0=ALU.mult)
                nc.sync.dma_start(out=out[b, ch * P : (ch + 1) * P, cols], in_=y[:])

        scalar_copy, vector_copy = nc.scalar.copy, nc.vector.tensor_copy


        lag = 2
        steps = B * PAIRS
        w_group()
        for n in range(steps):
            (nb, nk), (ob, ok) = divmod(n, PAIRS), divmod(n - lag, PAIRS)
            if n >= lag:
                score_pair(ob, ok)
            ride()
            if n == PAIRS + lag:
                riders.extend(log_steps(0) + [lambda: dust_gap(0)])
            if lag < n <= PAIRS + lag:
                turn_scores(0, 2 * (n - lag - 1))
                turn_scores(0, 2 * (n - lag - 1) + 1)
            for a in range(2):
                h_widen(nb, 2 * nk + a)
                ride()
            if n == lag - 1:
                w_quant()
            h_turn(nb, nk)
            if n >= lag:
                for a in range(2):
                    row_copy(ob, 2 * ok + a)
                    ride()
            if n == steps - 1:
                h_group(nb, nk)
            if n >= lag:
                row_sums(ob, ok)
            if n < steps - 1:
                h_group(nb, nk)
            if n > 0:
                f_parts(1 if n >= lag else 2, scalar_copy)

        score_pair(1, 2)
        ride()
        add_lse(0, 0, 0)
        f_quant(0, 0)
        score_pair(1, 3)
        ride()
        add_lse(0, 0, 1)
        for k in (2, 3):
            row_copy(1, 2 * k)
            row_copy(1, 2 * k + 1)
            row_sums(1, k)
            if k == 2:
                f_parts(1, scalar_copy)
                f_parts(2, vector_copy)
        add_lse(0, 1, 0)
        add_lse(0, 1, 1)
        dust_min(0, 6)

        col_least(0, 0, 0)
        riders.extend(log_steps(1))
        ride()
        f_parts(1, scalar_copy)
        ride()
        col_least(0, 0, 1)
        ride()
        for i in range(TILES):
            turn_scores(1, i)
        col_exp(0, 0)
        ride()
        dust_exp(0)
        ride()
        for q in range(PASSES):
            col_least(0, 1, q)
            ride()
        col_join(0, 0, 0)
        col_exp(0, 1)
        ride()
        col_invert(0, 0, 0)
        col_scale(0, 0)
        dust_turn(0)
        ride()
        dust_sum(0)
        ride()
        add_lse(1, 0, 0)
        add_lse(1, 0, 1)
        f_quant(0, 1)
        f_quant(1, 0)
        col_join(0, 0, 1)
        dust_gap(1)
        dust_invert(0)
        col_invert(0, 0, 1)
        col_scale(0, 1)
        f_parts(1, scalar_copy)
        dust_scale(0, 1)

        fold(0, 0, 0)
        add_lse(1, 1, 0)
        add_lse(1, 1, 1)
        fold(0, 1, 0)
        dust_min(1, 3)
        fold(0, 0, 1)
        fold(0, 1, 1)
        col_least(1, 0, 0)
        col_least(1, 0, 1)
        f_parts(1, vector_copy)
        col_exp(1, 0)
        col_least(1, 1, 0)
        col_least(1, 1, 1)
        row2_reduce(0, 0)
        col_exp(1, 1)
        dust_exp(1)
        row2_add_dust(0, 0)
        row2_reduce(0, 1)
        row2_invert(0, 0)
        col_join(1, 0, 0)
        row2_add_dust(0, 1)
        col_invert(1, 0, 0)
        col_scale(1, 0)
        row2_invert(0, 1)
        col_join(1, 0, 1)
        dust_turn(1)
        col_invert(1, 0, 1)
        col_scale(1, 1)
        f_parts(1, scalar_copy)

        col2_sum(0, 0, 0)
        dust_sum(1)
        fold(1, 0, 0)
        col2_sum(0, 0, 1)
        dust_invert(1)
        fold(1, 1, 0)
        col2_sum(0, 1, 0)
        dust_scale(1, P)
        col_join(0, 1, 0)
        fold(1, 0, 1)
        fold(1, 1, 1)
        row2_on_scalar(1, 0)
        row2_on_scalar(1, 1)
        col2_sum(0, 1, 1)
        col_invert(0, 1, 0)
        col_join(0, 1, 1)
        assign(0, 0, 0)
        col_invert(0, 1, 1)
        p_turn(0, 0, 0)
        assign(0, 0, 1)
        row2_invert(1, 0)
        p_turn(0, 0, 1)
        p_group(0, 0, 0)
        f_parts(1, scalar_copy)
        p_group(0, 0, 1)
        assign(0, 1, 0)
        row2_invert(1, 1)
        assign(0, 1, 1)
        p_move(0, 1, 0)
        p_move(0, 1, 1)

        col2_sum(1, 0, 0)
        aggregate(0, 0, 0)
        aggregate(0, 0, 1)
        col2_sum(1, 0, 1)
        aggregate(0, 1, 0)
        col_join(1, 1, 0)
        col2_sum(1, 1, 0)
        col_invert(1, 1, 0)
        aggregate(0, 1, 1)
        norm_square(0, 0)
        col2_sum(1, 1, 1)
        norm_root(0, 0)
        assign(1, 0, 0)
        col_join(1, 1, 1)
        p_move(1, 0, 0)
        assign(1, 0, 1)
        col_invert(1, 1, 1)
        p_move(1, 0, 1)
        norm_square(0, 1)
        assign(1, 1, 0)
        aggregate(1, 0, 0)
        p_move(1, 1, 0)
        norm_root(0, 1)
        assign(1, 1, 1)
        p_move(1, 1, 1)

        store(0, 0, on_scalar=True)
        f_quant(1, 1)
        aggregate(1, 0, 1)
        aggregate(1, 1, 0)
        aggregate(1, 1, 1)
        norm_square(1, 0)
        store(0, 1)
        norm_root(1, 0)
        norm_square(1, 1)
        store(1, 0)
        norm_root(1, 1)
        store(1, 1, parts=2)
